import numpy as np
import ml_dtypes


def mxq(x, axis, fmt="e4m3"):
    dtype, down = {"e4m3": (ml_dtypes.float8_e4m3fn, 7), "e5m2": (ml_dtypes.float8_e5m2, 14)}[fmt]
    v = np.moveaxis(np.asarray(x, np.float32).astype(ml_dtypes.bfloat16).astype(np.float64), axis, -1)
    blocks = v.reshape(v.shape[:-1] + (-1, 32))
    amax = np.abs(blocks).max(-1, keepdims=True)
    byte = np.maximum(np.where(amax > 0, np.frexp(amax)[1] - 1 + 127, 0) - down, 1)
    scale = np.exp2(byte - 127.0)
    codes = (blocks / scale).astype(np.float32).astype(dtype).astype(np.float64)
    return np.moveaxis((codes * scale).reshape(v.shape), -1, axis)


WIDE = False


def mx_kscale(k):
    if not WIDE:
        return np.ones(k)
    levels = np.array([10, -10, 5, -5, 0])
    if k % 512:
        return np.exp2(np.random.permutation(np.resize(levels, k // 32))).repeat(32)
    a = np.empty((k // 512, 16))
    for p in range(k // 512):
        a[p, :8] = np.random.permutation(np.resize(levels, 8))
        for g in range(8):
            far = levels[np.abs(levels - a[p, g]) >= 10]
            a[p, g + 8] = far[np.random.randint(len(far))]
    return np.exp2(a.ravel()).repeat(32)


BF16 = ml_dtypes.bfloat16


def bf(x):
    return np.asarray(x, np.float32).astype(BF16)


def f64(x):
    return np.asarray(x).astype(np.float64)


E2M1 = np.array([0.0, 0.5, 1.0, 1.5, 2.0, 3.0, 4.0, 6.0, -0.0, -0.5, -1.0, -1.5, -2.0, -3.0, -4.0, -6.0])


def pack_weight(w, fmt):
    k, n = w.shape
    w = f64(bf(w)).reshape(k // 32, 32, n)
    amax = np.abs(w).max(1)
    if fmt == "e4m3":
        byte = np.frexp(amax)[1] - 1 + 127 - 7
    else:
        mant, ex = np.frexp(amax / 6.0)
        byte = np.where(mant > 0.5, ex, ex - 1) + 127
    byte = np.clip(np.where(amax > 0, byte, 1), 1, 254)
    scaled = (w * np.exp2(127.0 - byte)[:, None, :]).reshape(k, n).astype(np.float32)
    by_word = np.ascontiguousarray(scaled.reshape(k // 512, 128, 4, n).transpose(0, 1, 3, 2))
    if fmt == "e4m3":
        words = by_word.astype(ml_dtypes.float8_e4m3fn).view(np.uint8)
    else:
        c = by_word.astype(ml_dtypes.float4_e2m1fn).view(np.uint8) & 0xF
        words = c[..., 0::2] | (c[..., 1::2] << 4)
    return np.ascontiguousarray(words), np.ascontiguousarray(byte.astype(np.uint8).reshape(k // 512, 16, n))


def unpack_weight(words, scales, fmt):
    g, p, n, _ = words.shape
    if fmt == "e4m3":
        vals = np.ascontiguousarray(words).view(ml_dtypes.float8_e4m3fn).astype(np.float64)
    else:
        nib = np.empty((g, p, n, 4), np.uint8)
        nib[..., 0::2] = words & 0xF
        nib[..., 1::2] = words >> 4
        vals = E2M1[nib]
    vals = vals * np.repeat(np.exp2(scales.astype(np.float64) - 127.0), 8, axis=1)[..., None]
    return vals.transpose(0, 1, 3, 2).reshape(g * 512, n)
def pack4(w):
    words, scales = pack_weight(w, "e2m1")
    return words.reshape(words.shape[0], 128, -1), scales


def unpack4(words, scales):
    return unpack_weight(words.reshape(words.shape[0], 128, -1, 2), scales, "e2m1")


M, FS, FR, D, N = 1024, 1024, 2048, 1024, 1536


def draw0():
    s, u, t = mx_kscale(FS), mx_kscale(FR), mx_kscale(D)
    hs = bf(np.random.standard_normal((M, FS)) * s)
    hr = bf(np.random.standard_normal((M, FR)) * u)
    gate = bf(np.random.uniform(0.4, 1.0, M))
    ws = bf(np.random.standard_normal((FS, D)) / np.sqrt(FS) / s[:, None])
    wr_words, wr_scales = pack4(np.random.standard_normal((FR, D)) / np.sqrt(FR) / u[:, None])
    gain = bf((1 + 0.1 * np.random.standard_normal(D)) * t)
    resid = bf(np.random.standard_normal((M, D)) * t)
    wo_words, wo_scales = pack4(np.random.standard_normal((D, N)) / np.sqrt(D) / t[:, None])
    return {"hs": hs, "hr": hr, "gate": gate, "ws": ws, "wr_words": wr_words, "wr_scales": wr_scales,
            "gain": gain, "resid": resid, "wo_words": wo_words, "wo_scales": wo_scales}


def core(hs, hr, gate, ws, wr_words, wr_scales, gain, resid, wo_words, wo_scales):
    routed = f64(hr) * f64(gate)[:, None]
    hs_q = mxq(f64(hs), 1, "e4m3")
    ws_q = mxq(f64(ws), 0, "e4m3")
    routed_q = mxq(routed, 1, "e4m3")
    wr = unpack4(wr_words, wr_scales)
    pair = (hs_q @ ws_q) + (routed_q @ wr)
    z = pair * f64(gain) + f64(resid)
    wo = unpack4(wo_words, wo_scales)
    return mxq(z, 1, "e4m3") @ wo


def e4m3fn_bytes(y):
    return np.clip(np.asarray(y, np.float64), -448.0, 448.0).astype(np.float32).astype(ml_dtypes.float8_e4m3fn).view(np.uint8)


def e4m3fn_values(b):
    return np.asarray(b, np.uint8).view(ml_dtypes.float8_e4m3fn).astype(np.float64)


def setup_inputs():
    d = draw0()
    x0 = np.asarray(d['ws']).astype(np.float64)
    s = (np.max(np.abs(x0), axis=(1,), keepdims=True) / 448.0).astype(np.float32)
    out = {}
    for k, v in d.items():
        if k == 'ws':
            out['ws_bytes'] = e4m3fn_bytes(x0 / s.astype(np.float64))
            out['ws_scale'] = s
        else:
            out[k] = v
    return out


def reference(hs, hr, gate, ws_bytes, ws_scale, wr_words, wr_scales, gain, resid, wo_words, wo_scales):
    return core(hs, hr, gate, e4m3fn_values(ws_bytes) * ws_scale.astype(np.float64), wr_words, wr_scales, gain, resid, wo_words, wo_scales)

@@ -1,0 +1,447 @@
+from contextlib import ExitStack
+
+import concourse.mybir as mybir
+from concourse.masks import make_identity
+
+TOKENS, SHARED, ROUTED, CHANNELS, FEATURES = 1024, 1024, 2048, 1024, 1536
+
+FLOPS = 2 * TOKENS * CHANNELS * (SHARED + ROUTED) + 2 * TOKENS * CHANNELS * FEATURES
+
+F32 = mybir.dt.float32
+BF16 = mybir.dt.bfloat16
+I32 = mybir.dt.int32
+U32 = mybir.dt.uint32
+U8 = mybir.dt.uint8
+FP8 = mybir.dt.float8_e4m3fn
+FP8X4 = mybir.dt.float8_e4m3fn_x4
+FP4X4 = mybir.dt.float4_e2m1fn_x4
+MULT = mybir.AluOpType.mult
+ADD = mybir.AluOpType.add
+COPY = mybir.ActivationFunctionType.Copy
+
+P = 128
+PACK = 4
+K_PASS = P * PACK
+UNIT = 2 * K_PASS
+BANK = 512
+BANKS = 8
+TILES = TOKENS // P
+R_PASSES = ROUTED // K_PASS
+S_PASSES = SHARED // K_PASS
+R_UNITS = ROUTED // UNIT
+HALVES = CHANNELS // BANK
+OUT_BANKS = FEATURES // BANK
+
+OPENING = 3
+LAG = 3
+
+
+def tile_expert_pair_project_s3_kernel(
+    tc, hs, hr, gate, ws_bytes, ws_scale, wr_words, wr_scales, gain, resid, wo_words, wo_scales, out
+):
+    nc = tc.nc
+    with ExitStack() as ctx:
+        keep = ctx.enter_context(tc.tile_pool(name="keep", bufs=1))
+        work = ctx.enter_context(tc.tile_pool(name="work", bufs=3))
+        psum = ctx.enter_context(tc.psum_pool(name="psum", bufs=1))
+        ctx.enter_context(tc.manual_schedule())
+
+        hs_rows = hs.rearrange("(p i) k -> p i k", i=TILES)
+        hr_rows = hr.rearrange("(p i) k -> p i k", i=TILES)
+        resid_rows = resid.rearrange("(p i) d -> p i d", i=TILES)
+        out_rows = out.rearrange("(p i) n -> p i n", i=TILES)
+
+        gate_sb = keep.tile([P, TILES], BF16, name="gate_sb")
+        gain_sb = keep.tile([P, CHANNELS], BF16, name="gain_sb")
+        hs_sb = [keep.tile([P, SHARED], BF16, name="hs%d" % i) for i in range(TILES)]
+        hr_sb = [keep.tile([P, ROUTED], BF16, name="hr%d" % i) for i in range(TILES)]
+        resid_sb = [keep.tile([P, CHANNELS], BF16, name="resid%d" % i) for i in range(TILES)]
+        wr_sb = keep.tile([P, R_PASSES, 2 * CHANNELS], U8, name="wr_sb", align_bytes=256)
+        wo_sb = keep.tile([P, HALVES, 2 * FEATURES], U8, name="wo_sb", align_bytes=256)
+        wr_planes = keep.tile([P, R_PASSES, CHANNELS // 4], I32, name="wr_planes", align_bytes=256)
+        wo_planes = keep.tile([P, HALVES, FEATURES // 4], I32, name="wo_planes", align_bytes=256)
+        ws_scale_sb = keep.tile([P, S_PASSES, PACK], F32, name="ws_scale_sb")
+        ws_raw = [keep.tile([P, PACK, CHANNELS], U8, name="ws_raw%d" % g) for g in range(S_PASSES)]
+
+        ws_wide = [keep.tile([P, PACK, CHANNELS], BF16, name="ws_wide%d" % g) for g in range(S_PASSES)]
+        ws_parts = [(g, h) for g in range(S_PASSES) for h in range(HALVES)]
+        ws_codes = {gh: keep.tile([P, BANK], U32, name="ws_codes%d%d" % gh, align_bytes=256) for gh in ws_parts}
+        ws_planes = {gh: keep.tile([P, BANK], U8, name="ws_planes%d%d" % gh, align_bytes=256) for gh in ws_parts}
+        ws_packed = {}
+
+        ident = keep.tile([P, P], F32, name="ident")
+        primer = keep.tile([P, 2], F32, name="primer")
+
+        units = {}
+        in_split_order = {}
+        turned = {}
+        grouped = {}
+        operands = {}
+        pair_banks = {}
+        scaled_pairs = {}
+        results = {}
+
+        def load_hr(i, cols=slice(0, ROUTED)):
+            nc.sync.dma_start(out=hr_sb[i][:, cols], in_=hr_rows[:, i, cols])
+
+        def load_hs(i):
+            nc.sync.dma_start(out=hs_sb[i][:], in_=hs_rows[:, i, :])
+
+        def load_resid(i):
+            nc.sync.dma_start(out=resid_sb[i][:], in_=resid_rows[:, i, :])
+
+        def load_ws(g, rows=slice(0, PACK)):
+            by_pass = ws_bytes.rearrange("(g p t) n -> g p t n", p=P, t=PACK)
+            nc.sync.dma_start(out=ws_raw[g][:, rows, :], in_=by_pass[g][:, rows, :])
+
+        def load_wr(g):
+            nc.sync.dma_start(out=wr_sb[:, g : g + 2, :], in_=wr_words[g : g + 2].rearrange("g p n -> p g n"))
+
+        def load_planes(planes, scales):
+            as_int = scales.bitcast(I32)
+            for r in range(4):
+                nc.sync.dma_start(out=planes[r:P:32, :, :], in_=as_int[:, r:16:4, :].rearrange("g q n -> q g n"))
+
+        def split(ap):
+            return ap.rearrange("p (w u e) -> p u w e", u=2, e=2)
+
+        def apply_gate(i, b):
+            routed = work.tile([P, UNIT], BF16, name="routed", bufs=6)
+            source = hr_sb[i][:, b * UNIT : (b + 1) * UNIT]
+            in_split_order["act", i, b] = i >= OPENING
+            if i >= OPENING:
+                target, source = routed[:].rearrange("p (u w e) -> p u w e", u=2, e=2), split(source)
+            else:
+                target = routed[:]
+            nc.vector.tensor_scalar(out=target, in0=source, scalar1=gate_sb[:, i : i + 1], scalar2=None, op0=MULT)
+            units["act", i, b] = routed
+
+        def order_hs(i):
+            ordered = work.tile([P, UNIT], BF16, name="ordered", bufs=4)
+            nc.scalar.copy(
+                out=ordered[:].bitcast(F32).rearrange("p (u w) -> p u w", u=2),
+                in_=hs_sb[i][:].bitcast(F32).rearrange("p (w u) -> p u w", u=2),
+            )
+            in_split_order["act", i, 2] = True
+            units["act", i, 2] = ordered
+
+        def bank_tile(k, shape):
+            return psum.tile(shape, F32, name="bank%d" % k)
+
+        def turn(key, k):
+            words = units[key][:].bitcast(F32)
+            bank = bank_tile(k, [P, 2, 2, P])
+            for g in range(2):
+                for u in range(2):
+                    if in_split_order[key]:
+                        block = words[:, (2 * u + g) * P : (2 * u + g + 1) * P]
+                    else:
+                        block = words[:, 2 * P * g + u : 2 * P * (g + 1) : 2]
+                    nc.tensor.transpose(bank[:, g, u, :], block, ident[:])
+            turned[key] = bank
+
+        def collect(key, copy):
+            rows = work.tile([P, UNIT], BF16, name="grouped", bufs=6, align_bytes=256)
+            copy(
+                out=rows[:].bitcast(F32).rearrange("p (g r u) -> p g r u", g=2, u=2),
+                in_=turned[key][:].rearrange("p g u r -> p g r u"),
+            )
+            grouped[key] = rows
+
+        def quantize(key):
+            codes = work.tile([P, 2 * P], U32, name="codes", bufs=12, align_bytes=256)
+            planes = work.tile([P, 2 * P], U8, name="planes", bufs=12, align_bytes=256)
+            nc.vector.quantize_mx(out=codes[:].bitcast(FP8X4), scales=planes[:], in_=grouped[key][:])
+            operands[key] = (codes, planes)
+
+        def stationary(key, g):
+            codes, planes = operands[key]
+            cols = slice(g * P, (g + 1) * P)
+            return codes[:, cols].bitcast(FP8X4), planes[:, cols]
+
+        def widen_on_vector(g, t):
+            nc.vector.tensor_scalar(
+                out=ws_wide[g][:, t, :],
+                in0=ws_raw[g][:, t, :].bitcast(FP8),
+                scalar1=ws_scale_sb[:, g, t : t + 1],
+                scalar2=None,
+                op0=MULT,
+            )
+
+        def widen_on_scalar(g, t):
+            nc.scalar.activation(
+                out=ws_wide[g][:, t, :],
+                in_=ws_raw[g][:, t, :].bitcast(FP8),
+                func=COPY,
+                scale=ws_scale_sb[:, g, t : t + 1],
+            )
+
+        def interleave(g, h, copy):
+            packed = work.tile([P, BANK, PACK], BF16, name="packed", bufs=4, align_bytes=256)
+            copy(out=packed[:], in_=ws_wide[g][:, :, h * BANK : (h + 1) * BANK].rearrange("p t n -> p n t"))
+            ws_packed[g, h] = packed
+
+        def quantize_ws(g, h):
+            nc.vector.quantize_mx(
+                out=ws_codes[g, h][:].bitcast(FP8X4),
+                scales=ws_planes[g, h][:],
+                in_=ws_packed[g, h][:].rearrange("p n t -> p (n t)"),
+            )
+
+        def open_pair(i, h, k):
+            pair_banks[i, h] = bank_tile(k, [P, BANK])
+
+        def routed_pass(i, h, g):
+            codes, planes = stationary(("act", i, g // 2), g % 2)
+            nc.tensor.matmul_mx(
+                out=pair_banks[i, h][:],
+                lhsT=codes,
+                lhsT_scale=planes,
+                rhs=wr_sb[:, g, 2 * h * BANK : 2 * (h + 1) * BANK].bitcast(FP4X4),
+                rhs_scale=wr_planes[:, g, h * BANK // 4 : (h + 1) * BANK // 4].bitcast(U8),
+                start=(g == 0),
+                stop=False,
+            )
+
+        def shared_pass(i, h, g):
+            codes, planes = stationary(("act", i, R_UNITS), g)
+            nc.tensor.matmul_mx(
+                out=pair_banks[i, h][:],
+                lhsT=codes,
+                lhsT_scale=planes,
+                rhs=ws_codes[g, h][:].bitcast(FP8X4),
+                rhs_scale=ws_planes[g, h][:],
+                start=False,
+                stop=(g == S_PASSES - 1),
+            )
+
+        def routed_unit(i, b):
+            for g in (2 * b, 2 * b + 1):
+                for h in range(HALVES):
+                    routed_pass(i, h, g)
+
+        def shared_unit(i):
+            for g in range(S_PASSES):
+                for h in range(HALVES):
+                    shared_pass(i, h, g)
+
+        def half_pair(i, h, k):
+            open_pair(i, h, k)
+            for g in range(R_PASSES):
+                routed_pass(i, h, g)
+            for g in range(S_PASSES):
+                shared_pass(i, h, g)
+
+        def scale_pair(i, h):
+            scaled = work.tile([P, BANK], F32, name="scaled", bufs=8)
+            channels = slice(h * BANK, (h + 1) * BANK)
+            nc.vector.tensor_tensor(out=scaled[:], in0=pair_banks[i, h][:], in1=gain_sb[:, channels], op=MULT)
+            scaled_pairs[i, h] = scaled
+
+        def add_resid(i, h):
+            if h == 0:
+                units["z", i] = work.tile([P, UNIT], BF16, name="z", bufs=4)
+                in_split_order["z", i] = True
+            nc.vector.tensor_tensor(
+                out=units["z", i][:].rearrange("p (u g w e) -> p g u w e", u=2, g=2, e=2)[:, h],
+                in0=split(scaled_pairs[i, h][:]),
+                in1=split(resid_sb[i][:, h * BANK : (h + 1) * BANK]),
+                op=ADD,
+            )
+
+        def project(i, n, k):
+            bank = bank_tile(k, [P, BANK])
+            for g in range(HALVES):
+                codes, planes = stationary(("z", i), g)
+                nc.tensor.matmul_mx(
+                    out=bank[:],
+                    lhsT=codes,
+                    lhsT_scale=planes,
+                    rhs=wo_sb[:, g, 2 * n * BANK : 2 * (n + 1) * BANK].bitcast(FP4X4),
+                    rhs_scale=wo_planes[:, g, n * BANK // 4 : (n + 1) * BANK // 4].bitcast(U8),
+                    start=(g == 0),
+                    stop=(g == HALVES - 1),
+                )
+            if n == 0:
+                results[i] = work.tile([P, FEATURES], F32, name="result", bufs=3)
+            copy = nc.vector.tensor_copy if i >= TILES - LAG and n == 1 else nc.scalar.copy
+            copy(out=results[i][:, n * BANK : (n + 1) * BANK], in_=bank[:])
+
+        def store(i, cols=slice(0, FEATURES)):
+            nc.sync.dma_start(out=out_rows[:, i, cols], in_=results[i][:, cols])
+
+        nc.vector.memset(primer[:], 0.0)
+        nc.vector.memset(wr_planes[:], 0)
+        nc.vector.memset(wo_planes[:], 0)
+        make_identity(nc, ident[:])
+        nc.scalar.activation(out=primer[:, 1:2], in_=primer[:, 0:1], func=COPY)
+
+        nc.sync.dma_start(out=gate_sb[:], in_=gate.rearrange("(p i) -> p i", i=TILES))
+        nc.sync.dma_start(out=ws_scale_sb[:], in_=ws_scale.rearrange("(g p t) o -> p g (t o)", p=P, t=PACK))
+        for b in range(2):
+            load_hr(0, slice(b * UNIT, (b + 1) * UNIT))
+            load_ws(0, slice(2 * b, 2 * b + 2))
+        load_hs(0)
+        load_hr(1)
+        load_planes(wr_planes, wr_scales)
+        load_wr(0)
+        load_ws(1)
+        load_wr(2)
+        load_hr(2)
+        load_hs(1)
+        load_hs(2)
+        load_hr(3)
+        load_hs(3)
+        nc.sync.dma_start(out=gain_sb[:], in_=gain.partition_broadcast(P))
+        load_resid(0)
+        load_hr(4)
+        load_hs(4)
+        load_planes(wo_planes, wo_scales)
+        nc.sync.dma_start(out=wo_sb[:], in_=wo_words.rearrange("g p n -> p g n"))
+        for i in range(5, TILES):
+            load_resid(i - 4)
+            load_hr(i)
+            load_hs(i)
+        for i in range(4, TILES):
+            load_resid(i)
+
+        on_vector, on_scalar = nc.vector.tensor_copy, nc.scalar.copy
+        for i in range(OPENING):
+            units["act", i, R_UNITS] = hs_sb[i]
+            in_split_order["act", i, R_UNITS] = False
+        pair_places = ((0, 3), (4, 5), (6, 7))
+
+        apply_gate(0, 0)
+        turn(("act", 0, 0), 1)
+        widen_on_scalar(0, 1)
+        widen_on_vector(0, 0)
+        collect(("act", 0, 0), on_scalar)
+        apply_gate(0, 1)
+        turn(("act", 0, 1), 2)
+        widen_on_vector(0, 2)
+        collect(("act", 0, 1), on_scalar)
+        turn(("act", 0, 2), 4)
+        quantize(("act", 0, 0))
+        widen_on_scalar(0, 3)
+        for b in range(R_UNITS):
+            apply_gate(1, b)
+            turn(("act", 1, b), 6 + b)
+        quantize(("act", 0, 1))
+        collect(("act", 0, 2), on_scalar)
+        interleave(0, 0, on_vector)
+        for b in range(R_UNITS):
+            collect(("act", 1, b), on_scalar)
+        interleave(0, 1, on_scalar)
+        for b in range(R_UNITS):
+            quantize(("act", 1, b))
+        for i in (0, 1):
+            for h in range(HALVES):
+                open_pair(i, h, pair_places[i][h])
+            routed_unit(i, 0)
+        for t in (3, 0, 2):
+            widen_on_vector(1, t)
+        for b in range(R_UNITS):
+            apply_gate(2, b)
+        widen_on_scalar(1, 1)
+        routed_unit(0, 1)
+        for b in range(R_UNITS):
+            turn(("act", 2, b), 1 + b)
+        routed_unit(1, 1)
+        turn(("act", 1, 2), 6)
+        turn(("act", 2, 2), 7)
+        interleave(1, 0, on_scalar)
+        for h in range(HALVES):
+            quantize_ws(0, h)
+        interleave(1, 1, on_vector)
+        quantize(("act", 0, 2))
+        for b in range(3):
+            collect(("act", 2, b), on_scalar)
+        for h in (1, 0):
+            quantize_ws(1, h)
+        quantize(("act", 2, 0))
+        collect(("act", 1, 2), on_vector)
+        quantize(("act", 2, 1))
+        shared_unit(0)
+        for h in range(HALVES):
+            open_pair(2, h, pair_places[2][h])
+        for b in range(R_UNITS):
+            routed_unit(2, b)
+        apply_gate(3, 0)
+        quantize(("act", 1, 2))
+        apply_gate(3, 1)
+        order_hs(3)
+        scale_pair(0, 0)
+        quantize(("act", 2, 2))
+        for b, k in enumerate((1, 2, 0)):
+            turn(("act", 3, b), k)
+            collect(("act", 3, b), on_scalar)
+        scale_pair(0, 1)
+        apply_gate(4, 0)
+        shared_unit(1)
+        add_resid(0, 0)
+        quantize(("act", 3, 0))
+        add_resid(0, 1)
+        shared_unit(2)
+        order_hs(4)
+        quantize(("act", 3, 1))
+        quantize(("act", 3, 2))
+        scale_pair(1, 0)
+        apply_gate(4, 1)
+        scale_pair(1, 1)
+        scale_pair(2, 0)
+
+        taken = []
+
+        def next_bank():
+            taken.append(len(taken) % BANKS)
+            return taken[-1]
+
+        def turn_next(key):
+            turn(key, next_bank())
+            collect(key, on_scalar)
+
+        last = TILES - 1
+        for i in range(OPENING, TILES):
+            half_pair(i, 0, next_bank())
+            scale_pair(i - 1, 1)
+            turn_next(("z", i - LAG))
+            if i < last:
+                for b in range(3):
+                    turn_next(("act", i + 1, b))
+            else:
+                turn_next(("z", i - LAG + 1))
+            scale_pair(i, 0)
+            quantize(("z", i - LAG))
+            if i < last:
+                for b in range(3):
+                    quantize(("act", i + 1, b))
+            half_pair(i, 1, next_bank())
+            if i + 2 < TILES:
+                order_hs(i + 2)
+            for n in range(OUT_BANKS):
+                project(i - LAG, n, next_bank())
+                if i == last:
+                    store(i - LAG, slice(n * BANK, (n + 1) * BANK))
+            if i < last:
+                store(i - LAG)
+            if i + 2 < TILES:
+                for b in range(R_UNITS):
+                    apply_gate(i + 2, b)
+            ready = {last - 1: (i - 2, i - 1), last: (i - 1,)}.get(i, (i - 2,))
+            for j in ready:
+                for h in range(HALVES):
+                    add_resid(j, h)
+
+        scale_pair(last, 1)
+        quantize(("z", last - 2))
+        turn_next(("z", last - 1))
+        for h in range(HALVES):
+            add_resid(last, h)
+        quantize(("z", last - 1))
+        for i in range(last - 2, TILES):
+            for n in range(OUT_BANKS):
+                project(i, n, next_bank())
+                store(i, slice(n * BANK, (n + 1) * BANK))
+            if i == last - 2:
+                turn_next(("z", last))
+                quantize(("z", last))

@@ -53,24 +53,26 @@ def tile_expert_pair_project_s3_kernel(
 
         gate_sb = keep.tile([P, TILES], BF16, name="gate_sb")
         gain_sb = keep.tile([P, CHANNELS], BF16, name="gain_sb")
-        hs_sb = [keep.tile([P, SHARED], BF16, name="hs%d" % i) for i in range(TILES)]
+        hs_pairs = [keep.tile([P, 2, SHARED], BF16, name="hs%d" % j) for j in range(TILES // 2)]
+        hs_sb = [hs_pairs[i // 2][:, i % 2, :] for i in range(TILES)]
         hr_sb = [keep.tile([P, ROUTED], BF16, name="hr%d" % i) for i in range(TILES)]
         resid_sb = [keep.tile([P, CHANNELS], BF16, name="resid%d" % i) for i in range(TILES)]
-        wr_sb = keep.tile([P, R_PASSES, 2 * CHANNELS], U8, name="wr_sb", align_bytes=256)
+        wr_sb = [keep.tile([P, 2 * CHANNELS], U8, name="wr%d" % g, align_bytes=256) for g in range(R_PASSES)]
         wo_sb = keep.tile([P, HALVES, 2 * FEATURES], U8, name="wo_sb", align_bytes=256)
-        wr_planes = keep.tile([P, R_PASSES, CHANNELS // 4], I32, name="wr_planes", align_bytes=256)
+        wr_planes = [
+            keep.tile([P, 2, CHANNELS // 4], I32, name="wr_planes%d" % b, align_bytes=256) for b in range(R_UNITS)
+        ]
         wo_planes = keep.tile([P, HALVES, FEATURES // 4], I32, name="wo_planes", align_bytes=256)
         ws_scale_sb = keep.tile([P, S_PASSES, PACK], F32, name="ws_scale_sb")
         ws_raw = [keep.tile([P, PACK, CHANNELS], U8, name="ws_raw%d" % g) for g in range(S_PASSES)]
 
-        ws_wide = [keep.tile([P, PACK, CHANNELS], BF16, name="ws_wide%d" % g) for g in range(S_PASSES)]
         ws_parts = [(g, h) for g in range(S_PASSES) for h in range(HALVES)]
+        ws_wide = {gh: keep.tile([P, PACK, BANK], BF16, name="ws_wide%d%d" % gh) for gh in ws_parts}
         ws_codes = {gh: keep.tile([P, BANK], U32, name="ws_codes%d%d" % gh, align_bytes=256) for gh in ws_parts}
         ws_planes = {gh: keep.tile([P, BANK], U8, name="ws_planes%d%d" % gh, align_bytes=256) for gh in ws_parts}
         ws_packed = {}
 
         ident = keep.tile([P, P], F32, name="ident")
-        primer = keep.tile([P, 2], F32, name="primer")
 
         units = {}
         in_split_order = {}
@@ -78,14 +80,15 @@ def tile_expert_pair_project_s3_kernel(
         grouped = {}
         operands = {}
         pair_banks = {}
+        passes_done = {}
         scaled_pairs = {}
         results = {}
 
         def load_hr(i, cols=slice(0, ROUTED)):
             nc.sync.dma_start(out=hr_sb[i][:, cols], in_=hr_rows[:, i, cols])
 
-        def load_hs(i):
-            nc.sync.dma_start(out=hs_sb[i][:], in_=hs_rows[:, i, :])
+        def load_hs(j):
+            nc.sync.dma_start(out=hs_pairs[j][:], in_=hs_rows[:, 2 * j : 2 * j + 2, :])
 
         def load_resid(i):
             nc.sync.dma_start(out=resid_sb[i][:], in_=resid_rows[:, i, :])
@@ -95,7 +98,7 @@ def tile_expert_pair_project_s3_kernel(
             nc.sync.dma_start(out=ws_raw[g][:, rows, :], in_=by_pass[g][:, rows, :])
 
         def load_wr(g):
-            nc.sync.dma_start(out=wr_sb[:, g : g + 2, :], in_=wr_words[g : g + 2].rearrange("g p n -> p g n"))
+            nc.sync.dma_start(out=wr_sb[g][:], in_=wr_words[g])
 
         def load_planes(planes, scales):
             as_int = scales.bitcast(I32)
@@ -108,17 +111,14 @@ def tile_expert_pair_project_s3_kernel(
         def apply_gate(i, b):
             routed = work.tile([P, UNIT], BF16, name="routed", bufs=6)
             source = hr_sb[i][:, b * UNIT : (b + 1) * UNIT]
-            in_split_order["act", i, b] = i >= OPENING
-            if i >= OPENING:
-                target, source = routed[:].rearrange("p (u w e) -> p u w e", u=2, e=2), split(source)
-            else:
-                target = routed[:]
+            in_split_order["act", i, b] = True
+            target, source = routed[:].rearrange("p (u w e) -> p u w e", u=2, e=2), split(source)
             nc.vector.tensor_scalar(out=target, in0=source, scalar1=gate_sb[:, i : i + 1], scalar2=None, op0=MULT)
             units["act", i, b] = routed
 
-        def order_hs(i):
+        def order_hs(i, copy):
             ordered = work.tile([P, UNIT], BF16, name="ordered", bufs=4)
-            nc.scalar.copy(
+            copy(
                 out=ordered[:].bitcast(F32).rearrange("p (u w) -> p u w", u=2),
                 in_=hs_sb[i][:].bitcast(F32).rearrange("p (w u) -> p u w", u=2),
             )
@@ -159,26 +159,28 @@ def tile_expert_pair_project_s3_kernel(
             cols = slice(g * P, (g + 1) * P)
             return codes[:, cols].bitcast(FP8X4), planes[:, cols]
 
-        def widen_on_vector(g, t):
+        def widen_on_vector(g, h, t):
+            cols = slice(h * BANK, (h + 1) * BANK)
             nc.vector.tensor_scalar(
-                out=ws_wide[g][:, t, :],
-                in0=ws_raw[g][:, t, :].bitcast(FP8),
+                out=ws_wide[g, h][:, t, :],
+                in0=ws_raw[g][:, t, cols].bitcast(FP8),
                 scalar1=ws_scale_sb[:, g, t : t + 1],
                 scalar2=None,
                 op0=MULT,
             )
 
-        def widen_on_scalar(g, t):
+        def widen_on_scalar(g, h, t):
+            cols = slice(h * BANK, (h + 1) * BANK)
             nc.scalar.activation(
-                out=ws_wide[g][:, t, :],
-                in_=ws_raw[g][:, t, :].bitcast(FP8),
+                out=ws_wide[g, h][:, t, :],
+                in_=ws_raw[g][:, t, cols].bitcast(FP8),
                 func=COPY,
                 scale=ws_scale_sb[:, g, t : t + 1],
             )
 
         def interleave(g, h, copy):
             packed = work.tile([P, BANK, PACK], BF16, name="packed", bufs=4, align_bytes=256)
-            copy(out=packed[:], in_=ws_wide[g][:, :, h * BANK : (h + 1) * BANK].rearrange("p t n -> p n t"))
+            copy(out=packed[:], in_=ws_wide[g, h][:].rearrange("p t n -> p n t"))
             ws_packed[g, h] = packed
 
         def quantize_ws(g, h):
@@ -191,19 +193,25 @@ def tile_expert_pair_project_s3_kernel(
         def open_pair(i, h, k):
             pair_banks[i, h] = bank_tile(k, [P, BANK])
 
+        def flags(i, h):
+            passes_done[i, h] = passes_done.get((i, h), 0) + 1
+            return passes_done[i, h] == 1, passes_done[i, h] == R_PASSES + S_PASSES
+
         def routed_pass(i, h, g):
+            start, stop = flags(i, h)
             codes, planes = stationary(("act", i, g // 2), g % 2)
             nc.tensor.matmul_mx(
                 out=pair_banks[i, h][:],
                 lhsT=codes,
                 lhsT_scale=planes,
-                rhs=wr_sb[:, g, 2 * h * BANK : 2 * (h + 1) * BANK].bitcast(FP4X4),
-                rhs_scale=wr_planes[:, g, h * BANK // 4 : (h + 1) * BANK // 4].bitcast(U8),
-                start=(g == 0),
-                stop=False,
+                rhs=wr_sb[g][:, 2 * h * BANK : 2 * (h + 1) * BANK].bitcast(FP4X4),
+                rhs_scale=wr_planes[g // 2][:, g % 2, h * BANK // 4 : (h + 1) * BANK // 4].bitcast(U8),
+                start=start,
+                stop=stop,
             )
 
         def shared_pass(i, h, g):
+            start, stop = flags(i, h)
             codes, planes = stationary(("act", i, R_UNITS), g)
             nc.tensor.matmul_mx(
                 out=pair_banks[i, h][:],
@@ -211,8 +219,8 @@ def tile_expert_pair_project_s3_kernel(
                 lhsT_scale=planes,
                 rhs=ws_codes[g, h][:].bitcast(FP8X4),
                 rhs_scale=ws_planes[g, h][:],
-                start=False,
-                stop=(g == S_PASSES - 1),
+                start=start,
+                stop=stop,
             )
 
         def routed_unit(i, b):
@@ -233,14 +241,14 @@ def tile_expert_pair_project_s3_kernel(
                 shared_pass(i, h, g)
 
         def scale_pair(i, h):
-            scaled = work.tile([P, BANK], F32, name="scaled", bufs=8)
+            scaled = work.tile([P, BANK], F32, name="scaled", bufs=6)
             channels = slice(h * BANK, (h + 1) * BANK)
             nc.vector.tensor_tensor(out=scaled[:], in0=pair_banks[i, h][:], in1=gain_sb[:, channels], op=MULT)
             scaled_pairs[i, h] = scaled
 
         def add_resid(i, h):
             if h == 0:
-                units["z", i] = work.tile([P, UNIT], BF16, name="z", bufs=4)
+                units["z", i] = work.tile([P, UNIT], BF16, name="z", bufs=5)
                 in_split_order["z", i] = True
             nc.vector.tensor_tensor(
                 out=units["z", i][:].rearrange("p (u g w e) -> p g u w e", u=2, g=2, e=2)[:, h],
@@ -270,130 +278,180 @@ def tile_expert_pair_project_s3_kernel(
         def store(i, cols=slice(0, FEATURES)):
             nc.sync.dma_start(out=out_rows[:, i, cols], in_=results[i][:, cols])
 
-        nc.vector.memset(primer[:], 0.0)
-        nc.vector.memset(wr_planes[:], 0)
+        for b in range(R_UNITS):
+            nc.vector.memset(wr_planes[b][:], 0)
         nc.vector.memset(wo_planes[:], 0)
         make_identity(nc, ident[:])
-        nc.scalar.activation(out=primer[:, 1:2], in_=primer[:, 0:1], func=COPY)
 
+        first, second = slice(0, UNIT), slice(UNIT, ROUTED)
         nc.sync.dma_start(out=gate_sb[:], in_=gate.rearrange("(p i) -> p i", i=TILES))
+        load_hr(0, first)
         nc.sync.dma_start(out=ws_scale_sb[:], in_=ws_scale.rearrange("(g p t) o -> p g (t o)", p=P, t=PACK))
-        for b in range(2):
-            load_hr(0, slice(b * UNIT, (b + 1) * UNIT))
-            load_ws(0, slice(2 * b, 2 * b + 2))
-        load_hs(0)
+        load_ws(0)
+        load_hr(0, second)
         load_hr(1)
-        load_planes(wr_planes, wr_scales)
-        load_wr(0)
-        load_ws(1)
-        load_wr(2)
         load_hr(2)
+        load_planes(wr_planes[0], wr_scales[0 : 2])
+        load_wr(0)
+        load_wr(1)
+        load_ws(1)
+        load_planes(wr_planes[1], wr_scales[2 : 4])
+        load_wr(2)
+        load_hs(0)
+        load_wr(3)
         load_hs(1)
-        load_hs(2)
         load_hr(3)
-        load_hs(3)
         nc.sync.dma_start(out=gain_sb[:], in_=gain.partition_broadcast(P))
         load_resid(0)
         load_hr(4)
-        load_hs(4)
+        load_hs(2)
+        load_resid(1)
         load_planes(wo_planes, wo_scales)
         nc.sync.dma_start(out=wo_sb[:], in_=wo_words.rearrange("g p n -> p g n"))
+        load_resid(2)
+        load_hr(5)
+        load_resid(3)
+        load_hr(6)
+        load_hs(3)
+        load_resid(4)
+        load_hr(7)
         for i in range(5, TILES):
-            load_resid(i - 4)
-            load_hr(i)
-            load_hs(i)
-        for i in range(4, TILES):
             load_resid(i)
 
         on_vector, on_scalar = nc.vector.tensor_copy, nc.scalar.copy
         for i in range(OPENING):
             units["act", i, R_UNITS] = hs_sb[i]
             in_split_order["act", i, R_UNITS] = False
-        pair_places = ((0, 3), (4, 5), (6, 7))
+        pair_places = ((2, 3), (4, 5), (6, 7))
 
-        apply_gate(0, 0)
-        turn(("act", 0, 0), 1)
-        widen_on_scalar(0, 1)
-        widen_on_vector(0, 0)
-        collect(("act", 0, 0), on_scalar)
-        apply_gate(0, 1)
-        turn(("act", 0, 1), 2)
-        widen_on_vector(0, 2)
-        collect(("act", 0, 1), on_scalar)
-        turn(("act", 0, 2), 4)
-        quantize(("act", 0, 0))
-        widen_on_scalar(0, 3)
-        for b in range(R_UNITS):
-            apply_gate(1, b)
-            turn(("act", 1, b), 6 + b)
-        quantize(("act", 0, 1))
-        collect(("act", 0, 2), on_scalar)
-        interleave(0, 0, on_vector)
-        for b in range(R_UNITS):
-            collect(("act", 1, b), on_scalar)
-        interleave(0, 1, on_scalar)
-        for b in range(R_UNITS):
-            quantize(("act", 1, b))
-        for i in (0, 1):
+        def open_tile(i):
             for h in range(HALVES):
                 open_pair(i, h, pair_places[i][h])
-            routed_unit(i, 0)
-        for t in (3, 0, 2):
-            widen_on_vector(1, t)
-        for b in range(R_UNITS):
-            apply_gate(2, b)
-        widen_on_scalar(1, 1)
-        routed_unit(0, 1)
-        for b in range(R_UNITS):
-            turn(("act", 2, b), 1 + b)
-        routed_unit(1, 1)
-        turn(("act", 1, 2), 6)
-        turn(("act", 2, 2), 7)
-        interleave(1, 0, on_scalar)
-        for h in range(HALVES):
-            quantize_ws(0, h)
-        interleave(1, 1, on_vector)
-        quantize(("act", 0, 2))
-        for b in range(3):
-            collect(("act", 2, b), on_scalar)
-        for h in (1, 0):
-            quantize_ws(1, h)
+
+        def routed_both(i, g):
+            for h in range(HALVES):
+                routed_pass(i, h, g)
+
+        def warm(count, k):
+            bank = bank_tile(k, [P, BANK])
+            for n in range(count):
+                nc.tensor.matmul(bank[:, 0:P], lhsT=ident[:], rhs=ident[:], start=True, stop=True)
+
+        apply_gate(0, 0)
+        turn(("act", 0, 0), 0)
+        widen_on_vector(0, 0, 0)
+        widen_on_vector(0, 0, 1)
+        widen_on_scalar(0, 0, 2)
+        collect(("act", 0, 0), on_scalar)
+        apply_gate(0, 1)
+        turn(("act", 0, 1), 1)
+        widen_on_scalar(0, 0, 3)
+        widen_on_vector(0, 1, 0)
+        widen_on_vector(0, 1, 1)
+        quantize(("act", 0, 0))
+        collect(("act", 0, 1), on_scalar)
+        apply_gate(1, 0)
+        apply_gate(1, 1)
+        turn(("act", 1, 0), 4)
+        turn(("act", 1, 1), 5)
+        widen_on_scalar(0, 1, 2)
+        quantize(("act", 0, 1))
+        apply_gate(2, 0)
+        apply_gate(2, 1)
+        collect(("act", 1, 0), on_scalar)
+        collect(("act", 1, 1), on_scalar)
+        turn(("act", 2, 0), 6)
+        turn(("act", 2, 1), 7)
+        interleave(0, 0, on_vector)
+        quantize(("act", 1, 0))
+        widen_on_scalar(0, 1, 3)
+        collect(("act", 2, 0), on_scalar)
+        collect(("act", 2, 1), on_scalar)
+        quantize(("act", 1, 1))
+        open_tile(0)
+        routed_both(0, 0)
+        open_tile(1)
+        routed_both(1, 0)
         quantize(("act", 2, 0))
-        collect(("act", 1, 2), on_vector)
+        quantize_ws(0, 0)
+        open_tile(2)
+        routed_both(2, 0)
+        routed_both(0, 1)
+        routed_both(1, 1)
+        routed_both(2, 1)
+        interleave(0, 1, on_vector)
+        widen_on_scalar(1, 0, 0)
+        widen_on_scalar(1, 0, 1)
+        widen_on_scalar(1, 0, 2)
+        widen_on_scalar(1, 0, 3)
         quantize(("act", 2, 1))
-        shared_unit(0)
-        for h in range(HALVES):
-            open_pair(2, h, pair_places[2][h])
-        for b in range(R_UNITS):
-            routed_unit(2, b)
+        quantize_ws(0, 1)
+        widen_on_vector(1, 1, 0)
+        widen_on_vector(1, 1, 1)
+        order_hs(0, on_vector)
+        order_hs(1, on_vector)
+        routed_both(0, 2)
+        routed_both(1, 2)
+        routed_both(2, 2)
+        widen_on_scalar(1, 1, 2)
+        widen_on_scalar(1, 1, 3)
+        interleave(1, 0, on_vector)
+        turn(("act", 0, 2), 0)
+        turn(("act", 1, 2), 1)
+        collect(("act", 0, 2), on_scalar)
+        collect(("act", 1, 2), on_scalar)
+        routed_both(0, 3)
+        routed_both(1, 3)
+        routed_both(2, 3)
+        order_hs(2, on_vector)
+        quantize_ws(1, 0)
         apply_gate(3, 0)
+        quantize(("act", 0, 2))
+        interleave(1, 1, on_vector)
+        turn(("act", 2, 2), 0)
+        turn(("act", 3, 0), 1)
         quantize(("act", 1, 2))
+        collect(("act", 2, 2), on_scalar)
+        collect(("act", 3, 0), on_scalar)
         apply_gate(3, 1)
-        order_hs(3)
-        scale_pair(0, 0)
+        quantize_ws(1, 1)
+        order_hs(3, on_scalar)
+        shared_pass(0, 0, 0)
+        shared_pass(0, 0, 1)
+        shared_pass(1, 0, 0)
+        shared_pass(1, 0, 1)
+        shared_pass(0, 1, 0)
+        shared_pass(0, 1, 1)
+        shared_pass(1, 1, 0)
+        shared_pass(1, 1, 1)
         quantize(("act", 2, 2))
-        for b, k in enumerate((1, 2, 0)):
-            turn(("act", 3, b), k)
-            collect(("act", 3, b), on_scalar)
-        scale_pair(0, 1)
-        apply_gate(4, 0)
-        shared_unit(1)
-        add_resid(0, 0)
+        scale_pair(0, 0)
+        turn(("act", 3, 1), 0)
+        turn(("act", 3, 2), 1)
+        collect(("act", 3, 1), on_scalar)
+        collect(("act", 3, 2), on_scalar)
         quantize(("act", 3, 0))
-        add_resid(0, 1)
-        shared_unit(2)
-        order_hs(4)
-        quantize(("act", 3, 1))
-        quantize(("act", 3, 2))
         scale_pair(1, 0)
+        shared_pass(2, 0, 0)
+        shared_pass(2, 1, 0)
+        shared_pass(2, 0, 1)
+        shared_pass(2, 1, 1)
+        scale_pair(0, 1)
+        add_resid(0, 0)
+        quantize(("act", 3, 1))
+        add_resid(0, 1)
+        quantize(("act", 3, 2))
+        apply_gate(4, 0)
         apply_gate(4, 1)
+        order_hs(4, on_scalar)
         scale_pair(1, 1)
         scale_pair(2, 0)
 
         taken = []
+        FIRST = (2, 0, 1, 4, 3, 5, 6, 7)
 
         def next_bank():
-            taken.append(len(taken) % BANKS)
+            taken.append((FIRST[len(taken)] if len(taken) < len(FIRST) else len(taken)) % BANKS)
             return taken[-1]
 
         def turn_next(key):
@@ -401,47 +459,52 @@ def tile_expert_pair_project_s3_kernel(
             collect(key, on_scalar)
 
         last = TILES - 1
-        for i in range(OPENING, TILES):
+        for i in range(OPENING, last):
             half_pair(i, 0, next_bank())
             scale_pair(i - 1, 1)
+            if i > OPENING:
+                add_resid(i - 1, 0)
             turn_next(("z", i - LAG))
-            if i < last:
-                for b in range(3):
-                    turn_next(("act", i + 1, b))
-            else:
-                turn_next(("z", i - LAG + 1))
+            for b in range(3):
+                turn_next(("act", i + 1, b))
             scale_pair(i, 0)
+            if i > OPENING:
+                add_resid(i - 1, 1)
             quantize(("z", i - LAG))
-            if i < last:
-                for b in range(3):
-                    quantize(("act", i + 1, b))
+            for b in range(3):
+                quantize(("act", i + 1, b))
             half_pair(i, 1, next_bank())
             if i + 2 < TILES:
-                order_hs(i + 2)
+                order_hs(i + 2, on_scalar)
             for n in range(OUT_BANKS):
                 project(i - LAG, n, next_bank())
-                if i == last:
-                    store(i - LAG, slice(n * BANK, (n + 1) * BANK))
-            if i < last:
-                store(i - LAG)
+            store(i - LAG)
             if i + 2 < TILES:
                 for b in range(R_UNITS):
                     apply_gate(i + 2, b)
-            ready = {last - 1: (i - 2, i - 1), last: (i - 1,)}.get(i, (i - 2,))
-            for j in ready:
-                for h in range(HALVES):
-                    add_resid(j, h)
+            if i == OPENING:
+                for j in (i - 2, i - 1):
+                    for h in range(HALVES):
+                        add_resid(j, h)
 
-        scale_pair(last, 1)
-        quantize(("z", last - 2))
-        turn_next(("z", last - 1))
+        half_pair(last, 0, next_bank())
+        scale_pair(last - 1, 1)
         for h in range(HALVES):
-            add_resid(last, h)
+            add_resid(last - 1, h)
+        for j in range(last - LAG, last):
+            turn_next(("z", j))
+        scale_pair(last, 0)
+        half_pair(last, 1, next_bank())
+        quantize(("z", last - 3))
+        add_resid(last, 0)
+        quantize(("z", last - 2))
+        scale_pair(last, 1)
         quantize(("z", last - 1))
-        for i in range(last - 2, TILES):
+        add_resid(last, 1)
+        for i in range(last - LAG, TILES):
+            if i == last - 1:
+                turn_next(("z", last))
+                quantize(("z", last))
             for n in range(OUT_BANKS):
                 project(i, n, next_bank())
                 store(i, slice(n * BANK, (n + 1) * BANK))
-            if i == last - 2:
-                turn_next(("z", last))
-                quantize(("z", last))

@@ -278,10 +278,13 @@ def tile_expert_pair_project_s3_kernel(
         def store(i, cols=slice(0, FEATURES)):
             nc.sync.dma_start(out=out_rows[:, i, cols], in_=results[i][:, cols])
 
+        primer = keep.tile([P, 2], F32, name="primer")
+        nc.vector.memset(primer[:], 0.0)
         for b in range(R_UNITS):
             nc.vector.memset(wr_planes[b][:], 0)
         nc.vector.memset(wo_planes[:], 0)
         make_identity(nc, ident[:])
+        nc.scalar.activation(out=primer[:, 1:2], in_=primer[:, 0:1], func=COPY)
 
         first, second = slice(0, UNIT), slice(UNIT, ROUTED)
         nc.sync.dma_start(out=gate_sb[:], in_=gate.rearrange("(p i) -> p i", i=TILES))

@@ -75,7 +75,7 @@ def tile_expert_pair_project_s3_kernel(
         ident = keep.tile([P, P], F32, name="ident")
 
         units = {}
-        in_split_order = {}
+        z_rows = {}
         turned = {}
         grouped = {}
         operands = {}
@@ -108,51 +108,60 @@ def tile_expert_pair_project_s3_kernel(
         def split(ap):
             return ap.rearrange("p (w u e) -> p u w e", u=2, e=2)
 
-        def apply_gate(i, b):
-            routed = work.tile([P, UNIT], BF16, name="routed", bufs=6)
-            source = hr_sb[i][:, b * UNIT : (b + 1) * UNIT]
-            in_split_order["act", i, b] = True
-            target, source = routed[:].rearrange("p (u w e) -> p u w e", u=2, e=2), split(source)
-            nc.vector.tensor_scalar(out=target, in0=source, scalar1=gate_sb[:, i : i + 1], scalar2=None, op0=MULT)
-            units["act", i, b] = routed
+        def apply_gate(i, parts=(0, 1)):
+            width = len(parts) * UNIT
+            routed = work.tile([P, ROUTED], BF16, name="routed", bufs=3)
+            source = hr_sb[i][:, parts[0] * UNIT : parts[0] * UNIT + width]
+            target = routed[:, 0:width].rearrange("p (u w e) -> p u w e", u=2, e=2)
+            nc.vector.tensor_scalar(
+                out=target, in0=split(source), scalar1=gate_sb[:, i : i + 1], scalar2=None, op0=MULT
+            )
+            words = routed[:, 0:width].bitcast(F32).rearrange("p (u w) -> p u w", u=2)
+            for n, b in enumerate(parts):
+                units["act", i, b] = words[:, :, 2 * P * n : 2 * P * (n + 1)]
 
         def order_hs(i, copy):
-            ordered = work.tile([P, UNIT], BF16, name="ordered", bufs=4)
-            copy(
-                out=ordered[:].bitcast(F32).rearrange("p (u w) -> p u w", u=2),
-                in_=hs_sb[i][:].bitcast(F32).rearrange("p (w u) -> p u w", u=2),
-            )
-            in_split_order["act", i, 2] = True
-            units["act", i, 2] = ordered
+            ordered = work.tile([P, 2, 2 * P], F32, name="ordered", bufs=3)
+            copy(out=ordered[:], in_=hs_sb[i].bitcast(F32).rearrange("p (w u) -> p u w", u=2))
+            units["act", i, R_UNITS] = ordered[:]
 
-        def bank_tile(k, shape):
-            return psum.tile(shape, F32, name="bank%d" % k)
+        def bank_tile(k, shape, dtype=F32):
+            return psum.tile(shape, dtype, name="bank%d" % k)
 
         def turn(key, k):
-            words = units[key][:].bitcast(F32)
             bank = bank_tile(k, [P, 2, 2, P])
             for g in range(2):
                 for u in range(2):
-                    if in_split_order[key]:
-                        block = words[:, (2 * u + g) * P : (2 * u + g + 1) * P]
-                    else:
-                        block = words[:, 2 * P * g + u : 2 * P * (g + 1) : 2]
-                    nc.tensor.transpose(bank[:, g, u, :], block, ident[:])
+                    nc.tensor.transpose(bank[:, g, u, :], units[key][:, u, g * P : (g + 1) * P], ident[:])
             turned[key] = bank
 
         def collect(key, copy):
-            rows = work.tile([P, UNIT], BF16, name="grouped", bufs=6, align_bytes=256)
+            if key[0] == "act" and key[2] < R_UNITS:
+                if key[2] == 0:
+                    grouped["routed", key[1]] = work.tile([P, ROUTED], BF16, name="grouped_r", bufs=3, align_bytes=256)
+                rows = grouped["routed", key[1]][:, key[2] * UNIT : (key[2] + 1) * UNIT]
+            else:
+                single = work.tile([P, UNIT], BF16, name="grouped", bufs=3, align_bytes=256)
+                rows = single[:]
             copy(
-                out=rows[:].bitcast(F32).rearrange("p (g r u) -> p g r u", g=2, u=2),
+                out=rows.bitcast(F32).rearrange("p (g r u) -> p g r u", g=2, u=2),
                 in_=turned[key][:].rearrange("p g u r -> p g r u"),
             )
             grouped[key] = rows
 
         def quantize(key):
-            codes = work.tile([P, 2 * P], U32, name="codes", bufs=12, align_bytes=256)
-            planes = work.tile([P, 2 * P], U8, name="planes", bufs=12, align_bytes=256)
-            nc.vector.quantize_mx(out=codes[:].bitcast(FP8X4), scales=planes[:], in_=grouped[key][:])
-            operands[key] = (codes, planes)
+            codes = work.tile([P, 2 * P], U32, name="codes", bufs=8, align_bytes=256)
+            planes = work.tile([P, 2 * P], U8, name="planes", bufs=8, align_bytes=256)
+            nc.vector.quantize_mx(out=codes[:].bitcast(FP8X4), scales=planes[:], in_=grouped[key])
+            operands[key] = (codes[:], planes[:])
+
+        def quantize_routed(i):
+            codes = work.tile([P, 4 * P], U32, name="codes_r", bufs=4, align_bytes=256)
+            planes = work.tile([P, 4 * P], U8, name="planes_r", bufs=4, align_bytes=256)
+            nc.vector.quantize_mx(out=codes[:].bitcast(FP8X4), scales=planes[:], in_=grouped["routed", i][:])
+            for b in range(R_UNITS):
+                cols = slice(2 * P * b, 2 * P * (b + 1))
+                operands["act", i, b] = (codes[:, cols], planes[:, cols])
 
         def stationary(key, g):
             codes, planes = operands[key]
@@ -178,10 +187,10 @@ def tile_expert_pair_project_s3_kernel(
                 scale=ws_scale_sb[:, g, t : t + 1],
             )
 
-        def interleave(g, h, copy):
-            packed = work.tile([P, BANK, PACK], BF16, name="packed", bufs=4, align_bytes=256)
-            copy(out=packed[:], in_=ws_wide[g, h][:].rearrange("p t n -> p n t"))
-            ws_packed[g, h] = packed
+        def interleave(g, h, copy, cols=slice(0, BANK)):
+            if (g, h) not in ws_packed:
+                ws_packed[g, h] = work.tile([P, BANK, PACK], BF16, name="packed", bufs=2, align_bytes=256)
+            copy(out=ws_packed[g, h][:, cols, :], in_=ws_wide[g, h][:, :, cols].rearrange("p t n -> p n t"))
 
         def quantize_ws(g, h):
             nc.vector.quantize_mx(
@@ -241,19 +250,24 @@ def tile_expert_pair_project_s3_kernel(
                 shared_pass(i, h, g)
 
         def scale_pair(i, h):
-            scaled = work.tile([P, BANK], F32, name="scaled", bufs=6)
+            if (i, 1 - h) not in scaled_pairs:
+                scaled_pairs[i] = work.tile([P, CHANNELS], F32, name="scaled", bufs=4)
+            scaled_pairs[i, h] = True
             channels = slice(h * BANK, (h + 1) * BANK)
-            nc.vector.tensor_tensor(out=scaled[:], in0=pair_banks[i, h][:], in1=gain_sb[:, channels], op=MULT)
-            scaled_pairs[i, h] = scaled
-
-        def add_resid(i, h):
-            if h == 0:
-                units["z", i] = work.tile([P, UNIT], BF16, name="z", bufs=5)
-                in_split_order["z", i] = True
             nc.vector.tensor_tensor(
-                out=units["z", i][:].rearrange("p (u g w e) -> p g u w e", u=2, g=2, e=2)[:, h],
-                in0=split(scaled_pairs[i, h][:]),
-                in1=split(resid_sb[i][:, h * BANK : (h + 1) * BANK]),
+                out=scaled_pairs[i][:, channels], in0=pair_banks[i, h][:], in1=gain_sb[:, channels], op=MULT
+            )
+
+        def add_resid(i, halves=(0, 1)):
+            if halves[0] == 0:
+                z_rows[i] = work.tile([P, UNIT], BF16, name="z", bufs=5)
+                units["z", i] = z_rows[i][:].bitcast(F32).rearrange("p (u w) -> p u w", u=2)
+            channels = slice(halves[0] * BANK, (halves[-1] + 1) * BANK)
+            words = slice(halves[0] * P, (halves[-1] + 1) * P)
+            nc.vector.tensor_tensor(
+                out=z_rows[i][:].rearrange("p (u w e) -> p u w e", u=2, e=2)[:, :, words, :],
+                in0=split(scaled_pairs[i][:, channels]),
+                in1=split(resid_sb[i][:, channels]),
                 op=ADD,
             )
 
@@ -323,8 +337,7 @@ def tile_expert_pair_project_s3_kernel(
 
         on_vector, on_scalar = nc.vector.tensor_copy, nc.scalar.copy
         for i in range(OPENING):
-            units["act", i, R_UNITS] = hs_sb[i]
-            in_split_order["act", i, R_UNITS] = False
+            units["act", i, R_UNITS] = hs_sb[i].bitcast(F32).rearrange("p (w u) -> p u w", u=2)
         pair_places = ((2, 3), (4, 5), (6, 7))
 
         def open_tile(i):
@@ -335,126 +348,136 @@ def tile_expert_pair_project_s3_kernel(
             for h in range(HALVES):
                 routed_pass(i, h, g)
 
-        def warm(count, k):
-            bank = bank_tile(k, [P, BANK])
-            for n in range(count):
-                nc.tensor.matmul(bank[:, 0:P], lhsT=ident[:], rhs=ident[:], start=True, stop=True)
-
-        apply_gate(0, 0)
+        apply_gate(0, (0,))
         turn(("act", 0, 0), 0)
         widen_on_vector(0, 0, 0)
+        widen_on_scalar(0, 1, 0)
         widen_on_vector(0, 0, 1)
-        widen_on_scalar(0, 0, 2)
         collect(("act", 0, 0), on_scalar)
-        apply_gate(0, 1)
+        apply_gate(0, (1,))
         turn(("act", 0, 1), 1)
-        widen_on_scalar(0, 0, 3)
-        widen_on_vector(0, 1, 0)
-        widen_on_vector(0, 1, 1)
+        widen_on_vector(0, 0, 2)
+        widen_on_scalar(0, 1, 1)
+        widen_on_vector(0, 0, 3)
+        apply_gate(1)
         quantize(("act", 0, 0))
         collect(("act", 0, 1), on_scalar)
-        apply_gate(1, 0)
-        apply_gate(1, 1)
         turn(("act", 1, 0), 4)
         turn(("act", 1, 1), 5)
         widen_on_scalar(0, 1, 2)
+        apply_gate(2)
         quantize(("act", 0, 1))
-        apply_gate(2, 0)
-        apply_gate(2, 1)
         collect(("act", 1, 0), on_scalar)
         collect(("act", 1, 1), on_scalar)
         turn(("act", 2, 0), 6)
         turn(("act", 2, 1), 7)
-        interleave(0, 0, on_vector)
         quantize(("act", 1, 0))
-        widen_on_scalar(0, 1, 3)
         collect(("act", 2, 0), on_scalar)
+        widen_on_scalar(0, 1, 3)
         collect(("act", 2, 1), on_scalar)
-        quantize(("act", 1, 1))
         open_tile(0)
         routed_both(0, 0)
+        routed_both(0, 1)
+        interleave(0, 0, on_vector)
         open_tile(1)
         routed_both(1, 0)
+        routed_both(1, 1)
         quantize(("act", 2, 0))
-        quantize_ws(0, 0)
         open_tile(2)
         routed_both(2, 0)
-        routed_both(0, 1)
-        routed_both(1, 1)
         routed_both(2, 1)
-        interleave(0, 1, on_vector)
         widen_on_scalar(1, 0, 0)
         widen_on_scalar(1, 0, 1)
         widen_on_scalar(1, 0, 2)
         widen_on_scalar(1, 0, 3)
+        quantize(("act", 1, 1))
+        quantize_ws(0, 0)
         quantize(("act", 2, 1))
-        quantize_ws(0, 1)
-        widen_on_vector(1, 1, 0)
-        widen_on_vector(1, 1, 1)
-        order_hs(0, on_vector)
-        order_hs(1, on_vector)
+        interleave(0, 1, on_vector)
         routed_both(0, 2)
         routed_both(1, 2)
         routed_both(2, 2)
-        widen_on_scalar(1, 1, 2)
-        widen_on_scalar(1, 1, 3)
+        widen_on_scalar(1, 1, 0)
+        widen_on_scalar(1, 1, 1)
         interleave(1, 0, on_vector)
         turn(("act", 0, 2), 0)
         turn(("act", 1, 2), 1)
+        widen_on_scalar(1, 1, 2)
+        widen_on_scalar(1, 1, 3)
         collect(("act", 0, 2), on_scalar)
         collect(("act", 1, 2), on_scalar)
         routed_both(0, 3)
         routed_both(1, 3)
         routed_both(2, 3)
-        order_hs(2, on_vector)
+        quantize_ws(0, 1)
         quantize_ws(1, 0)
-        apply_gate(3, 0)
+        apply_gate(3)
         quantize(("act", 0, 2))
-        interleave(1, 1, on_vector)
+        quantize(("act", 1, 2))
+        interleave(1, 1, on_scalar, slice(0, BANK // 2))
+        interleave(1, 1, on_vector, slice(BANK // 2, BANK))
         turn(("act", 2, 2), 0)
         turn(("act", 3, 0), 1)
-        quantize(("act", 1, 2))
         collect(("act", 2, 2), on_scalar)
         collect(("act", 3, 0), on_scalar)
-        apply_gate(3, 1)
-        quantize_ws(1, 1)
         order_hs(3, on_scalar)
         shared_pass(0, 0, 0)
+        shared_pass(0, 1, 0)
         shared_pass(0, 0, 1)
         shared_pass(1, 0, 0)
-        shared_pass(1, 0, 1)
-        shared_pass(0, 1, 0)
-        shared_pass(0, 1, 1)
         shared_pass(1, 1, 0)
-        shared_pass(1, 1, 1)
+        shared_pass(1, 0, 1)
+        quantize_ws(1, 1)
         quantize(("act", 2, 2))
         scale_pair(0, 0)
         turn(("act", 3, 1), 0)
         turn(("act", 3, 2), 1)
         collect(("act", 3, 1), on_scalar)
         collect(("act", 3, 2), on_scalar)
-        quantize(("act", 3, 0))
-        scale_pair(1, 0)
         shared_pass(2, 0, 0)
         shared_pass(2, 1, 0)
         shared_pass(2, 0, 1)
+        shared_pass(0, 1, 1)
+        shared_pass(1, 1, 1)
         shared_pass(2, 1, 1)
-        scale_pair(0, 1)
-        add_resid(0, 0)
-        quantize(("act", 3, 1))
-        add_resid(0, 1)
+        scale_pair(1, 0)
+        add_resid(0, (0,))
+        quantize_routed(3)
         quantize(("act", 3, 2))
-        apply_gate(4, 0)
-        apply_gate(4, 1)
+        scale_pair(0, 1)
+        apply_gate(4)
         order_hs(4, on_scalar)
-        scale_pair(1, 1)
+        add_resid(0, (1,))
+        half_pair(3, 0, 2)
+        turn(("act", 4, 0), 1)
+        turn(("z", 0), 0)
+        turn(("act", 4, 1), 4)
+        turn(("act", 4, 2), 3)
+        collect(("act", 4, 0), on_scalar)
+        collect(("z", 0), on_scalar)
+        collect(("act", 4, 1), on_scalar)
+        collect(("act", 4, 2), on_scalar)
         scale_pair(2, 0)
+        scale_pair(1, 1)
+        quantize(("z", 0))
+        half_pair(3, 1, 6)
+        scale_pair(2, 1)
+        scale_pair(3, 0)
+        quantize_routed(4)
+        order_hs(5, on_scalar)
+        project(0, 0, 5)
+        project(0, 1, 7)
+        project(0, 2, 0)
+        store(0)
+        quantize(("act", 4, 2))
+        add_resid(1)
+        apply_gate(5)
 
         taken = []
-        FIRST = (2, 0, 1, 4, 3, 5, 6, 7)
+        ring = (1, 4, 3, 2, 5, 7, 0, 6)
 
         def next_bank():
-            taken.append((FIRST[len(taken)] if len(taken) < len(FIRST) else len(taken)) % BANKS)
+            taken.append(ring[len(taken) % BANKS])
             return taken[-1]
 
         def turn_next(key):
@@ -462,51 +485,47 @@ def tile_expert_pair_project_s3_kernel(
             collect(key, on_scalar)
 
         last = TILES - 1
-        for i in range(OPENING, last):
+        for i in range(OPENING + 1, last):
             half_pair(i, 0, next_bank())
             scale_pair(i - 1, 1)
-            if i > OPENING:
-                add_resid(i - 1, 0)
             turn_next(("z", i - LAG))
             for b in range(3):
                 turn_next(("act", i + 1, b))
             scale_pair(i, 0)
-            if i > OPENING:
-                add_resid(i - 1, 1)
             quantize(("z", i - LAG))
-            for b in range(3):
-                quantize(("act", i + 1, b))
+            add_resid(i - 2 if i == OPENING + 1 else i - 1)
+            quantize_routed(i + 1)
             half_pair(i, 1, next_bank())
+            quantize(("act", i + 1, R_UNITS))
             if i + 2 < TILES:
                 order_hs(i + 2, on_scalar)
             for n in range(OUT_BANKS):
                 project(i - LAG, n, next_bank())
             store(i - LAG)
             if i + 2 < TILES:
-                for b in range(R_UNITS):
-                    apply_gate(i + 2, b)
-            if i == OPENING:
-                for j in (i - 2, i - 1):
-                    for h in range(HALVES):
-                        add_resid(j, h)
+                apply_gate(i + 2)
+            if i == OPENING + 1:
+                add_resid(i - 1)
+            if i == last - 1:
+                add_resid(i, (0,))
 
         half_pair(last, 0, next_bank())
         scale_pair(last - 1, 1)
-        for h in range(HALVES):
-            add_resid(last - 1, h)
+        add_resid(last - 1, (1,))
         for j in range(last - LAG, last):
             turn_next(("z", j))
         scale_pair(last, 0)
         half_pair(last, 1, next_bank())
         quantize(("z", last - 3))
-        add_resid(last, 0)
+        add_resid(last, (0,))
         quantize(("z", last - 2))
         scale_pair(last, 1)
         quantize(("z", last - 1))
-        add_resid(last, 1)
+        add_resid(last, (1,))
         for i in range(last - LAG, TILES):
             if i == last - 1:
-                turn_next(("z", last))
+                turn(("z", last), next_bank())
+                collect(("z", last), on_vector)
                 quantize(("z", last))
             for n in range(OUT_BANKS):
                 project(i, n, next_bank())

@@ -348,14 +348,24 @@ def tile_expert_pair_project_s3_kernel(
             for h in range(HALVES):
                 routed_pass(i, h, g)
 
+        twice = ident[:].unsqueeze(1).to_broadcast([P, 2, P])
+
+        def warm(count, k):
+            bank = bank_tile(k, [P, BANK])
+            for n in range(count):
+                nc.tensor.matmul(bank[:, 0 : 2 * P], lhsT=ident[:], rhs=twice, start=True, stop=True)
+
+        warm(2, 7)
         apply_gate(0, (0,))
         turn(("act", 0, 0), 0)
+        warm(1, 7)
         widen_on_vector(0, 0, 0)
         widen_on_scalar(0, 1, 0)
         widen_on_vector(0, 0, 1)
         collect(("act", 0, 0), on_scalar)
         apply_gate(0, (1,))
         turn(("act", 0, 1), 1)
+        warm(2, 7)
         widen_on_vector(0, 0, 2)
         widen_on_scalar(0, 1, 1)
         widen_on_vector(0, 0, 3)

@@ -64,7 +64,9 @@ def tile_expert_pair_project_s3_kernel(
         ]
         wo_planes = keep.tile([P, HALVES, FEATURES // 4], I32, name="wo_planes", align_bytes=256)
         ws_scale_sb = keep.tile([P, S_PASSES, PACK], F32, name="ws_scale_sb")
-        ws_raw = [keep.tile([P, PACK, CHANNELS], U8, name="ws_raw%d" % g) for g in range(S_PASSES)]
+        ws_raw = [
+            [keep.tile([P, 2, CHANNELS], U8, name="ws_raw%d%d" % (g, j)) for j in range(2)] for g in range(S_PASSES)
+        ]
 
         ws_parts = [(g, h) for g in range(S_PASSES) for h in range(HALVES)]
         ws_wide = {gh: keep.tile([P, PACK, BANK], BF16, name="ws_wide%d%d" % gh) for gh in ws_parts}
@@ -82,6 +84,7 @@ def tile_expert_pair_project_s3_kernel(
         pair_banks = {}
         passes_done = {}
         scaled_pairs = {}
+        out_banks = {}
         results = {}
 
         def load_hr(i, cols=slice(0, ROUTED)):
@@ -93,9 +96,9 @@ def tile_expert_pair_project_s3_kernel(
         def load_resid(i):
             nc.sync.dma_start(out=resid_sb[i][:], in_=resid_rows[:, i, :])
 
-        def load_ws(g, rows=slice(0, PACK)):
+        def load_ws(g, j):
             by_pass = ws_bytes.rearrange("(g p t) n -> g p t n", p=P, t=PACK)
-            nc.sync.dma_start(out=ws_raw[g][:, rows, :], in_=by_pass[g][:, rows, :])
+            nc.sync.dma_start(out=ws_raw[g][j][:], in_=by_pass[g][:, 2 * j : 2 * j + 2, :])
 
         def load_wr(g):
             nc.sync.dma_start(out=wr_sb[g][:], in_=wr_words[g])
@@ -112,9 +115,12 @@ def tile_expert_pair_project_s3_kernel(
             width = len(parts) * UNIT
             routed = work.tile([P, ROUTED], BF16, name="routed", bufs=3)
             source = hr_sb[i][:, parts[0] * UNIT : parts[0] * UNIT + width]
-            target = routed[:, 0:width].rearrange("p (u w e) -> p u w e", u=2, e=2)
             nc.vector.tensor_scalar(
-                out=target, in0=split(source), scalar1=gate_sb[:, i : i + 1], scalar2=None, op0=MULT
+                out=routed[:, 0:width].rearrange("p (u w e) -> p w u e", u=2, e=2),
+                in0=source.rearrange("p (w u e) -> p w u e", u=2, e=2),
+                scalar1=gate_sb[:, i : i + 1],
+                scalar2=None,
+                op0=MULT,
             )
             words = routed[:, 0:width].bitcast(F32).rearrange("p (u w) -> p u w", u=2)
             for n, b in enumerate(parts):
@@ -122,7 +128,7 @@ def tile_expert_pair_project_s3_kernel(
 
         def order_hs(i, copy):
             ordered = work.tile([P, 2, 2 * P], F32, name="ordered", bufs=3)
-            copy(out=ordered[:], in_=hs_sb[i].bitcast(F32).rearrange("p (w u) -> p u w", u=2))
+            copy(out=ordered[:].rearrange("p u w -> p w u"), in_=hs_sb[i].bitcast(F32).rearrange("p (w u) -> p w u", u=2))
             units["act", i, R_UNITS] = ordered[:]
 
         def bank_tile(k, shape, dtype=F32):
@@ -172,7 +178,7 @@ def tile_expert_pair_project_s3_kernel(
             cols = slice(h * BANK, (h + 1) * BANK)
             nc.vector.tensor_scalar(
                 out=ws_wide[g, h][:, t, :],
-                in0=ws_raw[g][:, t, cols].bitcast(FP8),
+                in0=ws_raw[g][t // 2][:, t % 2, cols].bitcast(FP8),
                 scalar1=ws_scale_sb[:, g, t : t + 1],
                 scalar2=None,
                 op0=MULT,
@@ -182,7 +188,7 @@ def tile_expert_pair_project_s3_kernel(
             cols = slice(h * BANK, (h + 1) * BANK)
             nc.scalar.activation(
                 out=ws_wide[g, h][:, t, :],
-                in_=ws_raw[g][:, t, cols].bitcast(FP8),
+                in_=ws_raw[g][t // 2][:, t % 2, cols].bitcast(FP8),
                 func=COPY,
                 scale=ws_scale_sb[:, g, t : t + 1],
             )
@@ -190,7 +196,10 @@ def tile_expert_pair_project_s3_kernel(
         def interleave(g, h, copy, cols=slice(0, BANK)):
             if (g, h) not in ws_packed:
                 ws_packed[g, h] = work.tile([P, BANK, PACK], BF16, name="packed", bufs=2, align_bytes=256)
-            copy(out=ws_packed[g, h][:, cols, :], in_=ws_wide[g, h][:, :, cols].rearrange("p t n -> p n t"))
+            copy(
+                out=ws_packed[g, h][:, cols, :].rearrange("p (c i) t -> p c t i", i=4),
+                in_=ws_wide[g, h][:, :, cols].rearrange("p t (c i) -> p c t i", i=4),
+            )
 
         def quantize_ws(g, h):
             nc.vector.quantize_mx(
@@ -271,23 +280,30 @@ def tile_expert_pair_project_s3_kernel(
                 op=ADD,
             )
 
-        def project(i, n, k):
-            bank = bank_tile(k, [P, BANK])
-            for g in range(HALVES):
-                codes, planes = stationary(("z", i), g)
-                nc.tensor.matmul_mx(
-                    out=bank[:],
-                    lhsT=codes,
-                    lhsT_scale=planes,
-                    rhs=wo_sb[:, g, 2 * n * BANK : 2 * (n + 1) * BANK].bitcast(FP4X4),
-                    rhs_scale=wo_planes[:, g, n * BANK // 4 : (n + 1) * BANK // 4].bitcast(U8),
-                    start=(g == 0),
-                    stop=(g == HALVES - 1),
-                )
-            if n == 0:
+        def project_pass(i, cols, g, k=None):
+            if g == 0:
+                out_banks[i, cols.start] = bank_tile(k, [P, cols.stop - cols.start])
+            codes, planes = stationary(("z", i), g)
+            nc.tensor.matmul_mx(
+                out=out_banks[i, cols.start][:],
+                lhsT=codes,
+                lhsT_scale=planes,
+                rhs=wo_sb[:, g, 2 * cols.start : 2 * cols.stop].bitcast(FP4X4),
+                rhs_scale=wo_planes[:, g, cols.start // 4 : cols.stop // 4].bitcast(U8),
+                start=(g == 0),
+                stop=(g == HALVES - 1),
+            )
+
+        def empty(i, cols, copy):
+            if cols.start == 0:
                 results[i] = work.tile([P, FEATURES], F32, name="result", bufs=3)
-            copy = nc.vector.tensor_copy if i >= TILES - LAG and n == 1 else nc.scalar.copy
-            copy(out=results[i][:, n * BANK : (n + 1) * BANK], in_=bank[:])
+            copy(out=results[i][:, cols], in_=out_banks[i, cols.start][:])
+
+        def project(i, n, k, copy=nc.scalar.copy):
+            cols = slice(n * BANK, (n + 1) * BANK)
+            for g in range(HALVES):
+                project_pass(i, cols, g, k)
+            empty(i, cols, copy)
 
         def store(i, cols=slice(0, FEATURES)):
             nc.sync.dma_start(out=out_rows[:, i, cols], in_=results[i][:, cols])
@@ -301,23 +317,26 @@ def tile_expert_pair_project_s3_kernel(
         nc.scalar.activation(out=primer[:, 1:2], in_=primer[:, 0:1], func=COPY)
 
         first, second = slice(0, UNIT), slice(UNIT, ROUTED)
+        nc.sync.dma_start(out=ws_scale_sb[:], in_=ws_scale.rearrange("(g p t) o -> p g (t o)", p=P, t=PACK))
+        load_ws(0, 0)
         nc.sync.dma_start(out=gate_sb[:], in_=gate.rearrange("(p i) -> p i", i=TILES))
         load_hr(0, first)
-        nc.sync.dma_start(out=ws_scale_sb[:], in_=ws_scale.rearrange("(g p t) o -> p g (t o)", p=P, t=PACK))
-        load_ws(0)
+        load_ws(0, 1)
         load_hr(0, second)
         load_hr(1)
         load_hr(2)
         load_planes(wr_planes[0], wr_scales[0 : 2])
         load_wr(0)
         load_wr(1)
-        load_ws(1)
+        load_ws(1, 0)
+        load_ws(1, 1)
         load_planes(wr_planes[1], wr_scales[2 : 4])
         load_wr(2)
         load_hs(0)
         load_wr(3)
         load_hs(1)
-        load_hr(3)
+        load_hr(3, first)
+        load_hr(3, second)
         nc.sync.dma_start(out=gain_sb[:], in_=gain.partition_broadcast(P))
         load_resid(0)
         load_hr(4)
@@ -336,7 +355,7 @@ def tile_expert_pair_project_s3_kernel(
             load_resid(i)
 
         on_vector, on_scalar = nc.vector.tensor_copy, nc.scalar.copy
-        for i in range(OPENING):
+        for i in range(OPENING + 1):
             units["act", i, R_UNITS] = hs_sb[i].bitcast(F32).rearrange("p (w u) -> p u w", u=2)
         pair_places = ((2, 3), (4, 5), (6, 7))
 
@@ -356,39 +375,43 @@ def tile_expert_pair_project_s3_kernel(
                 nc.tensor.matmul(bank[:, 0 : 2 * P], lhsT=ident[:], rhs=twice, start=True, stop=True)
 
         warm(2, 7)
-        apply_gate(0, (0,))
-        turn(("act", 0, 0), 0)
-        warm(1, 7)
         widen_on_vector(0, 0, 0)
         widen_on_scalar(0, 1, 0)
         widen_on_vector(0, 0, 1)
+        apply_gate(0, (0,))
+        turn(("act", 0, 0), 0)
+        warm(1, 7)
+        widen_on_scalar(0, 1, 1)
+        widen_on_vector(0, 0, 2)
         collect(("act", 0, 0), on_scalar)
+        widen_on_vector(0, 0, 3)
         apply_gate(0, (1,))
         turn(("act", 0, 1), 1)
-        warm(2, 7)
-        widen_on_vector(0, 0, 2)
-        widen_on_scalar(0, 1, 1)
-        widen_on_vector(0, 0, 3)
-        apply_gate(1)
-        quantize(("act", 0, 0))
+        warm(1, 7)
+        widen_on_scalar(0, 1, 2)
+        interleave(0, 0, on_vector, slice(0, BANK // 2))
+        apply_gate(1, (0,))
+        apply_gate(1, (1,))
         collect(("act", 0, 1), on_scalar)
         turn(("act", 1, 0), 4)
         turn(("act", 1, 1), 5)
-        widen_on_scalar(0, 1, 2)
-        apply_gate(2)
-        quantize(("act", 0, 1))
+        warm(1, 3)
+        widen_on_scalar(0, 1, 3)
+        quantize(("act", 0, 0))
+        apply_gate(2, (0,))
+        apply_gate(2, (1,))
         collect(("act", 1, 0), on_scalar)
         collect(("act", 1, 1), on_scalar)
         turn(("act", 2, 0), 6)
         turn(("act", 2, 1), 7)
+        quantize(("act", 0, 1))
         quantize(("act", 1, 0))
         collect(("act", 2, 0), on_scalar)
-        widen_on_scalar(0, 1, 3)
         collect(("act", 2, 1), on_scalar)
+        interleave(0, 0, on_vector, slice(BANK // 2, BANK))
         open_tile(0)
         routed_both(0, 0)
         routed_both(0, 1)
-        interleave(0, 0, on_vector)
         open_tile(1)
         routed_both(1, 0)
         routed_both(1, 1)
@@ -400,10 +423,12 @@ def tile_expert_pair_project_s3_kernel(
         widen_on_scalar(1, 0, 1)
         widen_on_scalar(1, 0, 2)
         widen_on_scalar(1, 0, 3)
-        quantize(("act", 1, 1))
-        quantize_ws(0, 0)
-        quantize(("act", 2, 1))
         interleave(0, 1, on_vector)
+        quantize(("act", 1, 1))
+        quantize(("act", 2, 1))
+        quantize_ws(0, 0)
+        order_hs(0, on_vector)
+        order_hs(1, on_vector)
         routed_both(0, 2)
         routed_both(1, 2)
         routed_both(2, 2)
@@ -413,33 +438,36 @@ def tile_expert_pair_project_s3_kernel(
         turn(("act", 0, 2), 0)
         turn(("act", 1, 2), 1)
         widen_on_scalar(1, 1, 2)
-        widen_on_scalar(1, 1, 3)
         collect(("act", 0, 2), on_scalar)
         collect(("act", 1, 2), on_scalar)
+        widen_on_scalar(1, 1, 3)
         routed_both(0, 3)
         routed_both(1, 3)
         routed_both(2, 3)
         quantize_ws(0, 1)
-        quantize_ws(1, 0)
-        apply_gate(3)
+        order_hs(2, on_vector)
+        apply_gate(3, (0,))
+        order_hs(3, on_vector)
         quantize(("act", 0, 2))
+        quantize_ws(1, 0)
         quantize(("act", 1, 2))
-        interleave(1, 1, on_scalar, slice(0, BANK // 2))
-        interleave(1, 1, on_vector, slice(BANK // 2, BANK))
         turn(("act", 2, 2), 0)
         turn(("act", 3, 0), 1)
+        interleave(1, 1, on_vector, slice(0, BANK // 2))
         collect(("act", 2, 2), on_scalar)
+        interleave(1, 1, on_scalar, slice(BANK // 2, BANK))
         collect(("act", 3, 0), on_scalar)
-        order_hs(3, on_scalar)
+        apply_gate(3, (1,))
         shared_pass(0, 0, 0)
         shared_pass(0, 1, 0)
         shared_pass(0, 0, 1)
         shared_pass(1, 0, 0)
         shared_pass(1, 1, 0)
         shared_pass(1, 0, 1)
-        quantize_ws(1, 1)
         quantize(("act", 2, 2))
         scale_pair(0, 0)
+        quantize_ws(1, 1)
+        scale_pair(1, 0)
         turn(("act", 3, 1), 0)
         turn(("act", 3, 2), 1)
         collect(("act", 3, 1), on_scalar)
@@ -450,13 +478,12 @@ def tile_expert_pair_project_s3_kernel(
         shared_pass(0, 1, 1)
         shared_pass(1, 1, 1)
         shared_pass(2, 1, 1)
-        scale_pair(1, 0)
-        add_resid(0, (0,))
         quantize_routed(3)
         quantize(("act", 3, 2))
         scale_pair(0, 1)
         apply_gate(4)
         order_hs(4, on_scalar)
+        add_resid(0, (0,))
         add_resid(0, (1,))
         half_pair(3, 0, 2)
         turn(("act", 4, 0), 1)
@@ -469,9 +496,9 @@ def tile_expert_pair_project_s3_kernel(
         collect(("act", 4, 2), on_scalar)
         scale_pair(2, 0)
         scale_pair(1, 1)
+        scale_pair(2, 1)
         quantize(("z", 0))
         half_pair(3, 1, 6)
-        scale_pair(2, 1)
         scale_pair(3, 0)
         quantize_routed(4)
         order_hs(5, on_scalar)
@@ -538,5 +565,5 @@ def tile_expert_pair_project_s3_kernel(
                 collect(("z", last), on_vector)
                 quantize(("z", last))
             for n in range(OUT_BANKS):
-                project(i, n, next_bank())
+                project(i, n, next_bank(), on_vector if i > last - LAG and n == 1 else on_scalar)
                 store(i, slice(n * BANK, (n + 1) * BANK))

@@ -33,6 +33,9 @@ HALVES = CHANNELS // BANK
 OUT_BANKS = FEATURES // BANK
 
 OPENING = 3
+QUAD = 32
+QUADS = P // QUAD
+ON_VECTOR = 6
 LAG = 3
 
 
@@ -55,7 +58,12 @@ def tile_expert_pair_project_s3_kernel(
         gain_sb = keep.tile([P, CHANNELS], BF16, name="gain_sb")
         hs_pairs = [keep.tile([P, 2, SHARED], BF16, name="hs%d" % j) for j in range(TILES // 2)]
         hs_sb = [hs_pairs[i // 2][:, i % 2, :] for i in range(TILES)]
-        hr_sb = [keep.tile([P, ROUTED], BF16, name="hr%d" % i) for i in range(TILES)]
+        hr_sb = [keep.tile([P, ROUTED], BF16, name="hr%d" % i) for i in range(ON_VECTOR)]
+        late = TILES - ON_VECTOR
+        hr_quads = [keep.tile([P, late * R_PASSES, P], BF16, name="hr_quad%d" % b) for b in range(QUADS)]
+        gate_quads = keep.tile([P, QUADS, TILES], BF16, name="gate_quads")
+        staged = {}
+        flipped = {}
         resid_sb = [keep.tile([P, CHANNELS], BF16, name="resid%d" % i) for i in range(TILES)]
         wr_sb = [keep.tile([P, 2 * CHANNELS], U8, name="wr%d" % g, align_bytes=256) for g in range(R_PASSES)]
         wo_sb = keep.tile([P, HALVES, 2 * FEATURES], U8, name="wo_sb", align_bytes=256)
@@ -90,6 +98,19 @@ def tile_expert_pair_project_s3_kernel(
         def load_hr(i, cols=slice(0, ROUTED)):
             nc.sync.dma_start(out=hr_sb[i][:, cols], in_=hr_rows[:, i, cols])
 
+        def load_quads(b):
+            pieces = hr.rearrange("(b r i) (g q c) -> q b r (i g) c", b=QUADS, r=QUAD, g=R_PASSES, q=QUADS)
+            for q in (0, 2, 1, 3):
+                nc.sync.dma_start(
+                    out=hr_quads[b][q * QUAD : (q + 1) * QUAD, :, :], in_=pieces[q, b][:, ON_VECTOR * R_PASSES :, :]
+                )
+
+        def load_gate_quads():
+            for q in range(QUADS):
+                nc.sync.dma_start(
+                    out=gate_quads[q * QUAD : (q + 1) * QUAD, :, :], in_=gate.rearrange("(b r i) -> r b i", b=QUADS, r=QUAD)
+                )
+
         def load_hs(j):
             nc.sync.dma_start(out=hs_pairs[j][:], in_=hs_rows[:, 2 * j : 2 * j + 2, :])
 
@@ -113,7 +134,7 @@ def tile_expert_pair_project_s3_kernel(
 
         def apply_gate(i, parts=(0, 1)):
             width = len(parts) * UNIT
-            routed = work.tile([P, ROUTED], BF16, name="routed", bufs=3)
+            routed = work.tile([P, ROUTED], BF16, name="routed", bufs=2)
             source = hr_sb[i][:, parts[0] * UNIT : parts[0] * UNIT + width]
             nc.vector.tensor_scalar(
                 out=routed[:, 0:width].rearrange("p (u w e) -> p w u e", u=2, e=2),
@@ -125,6 +146,31 @@ def tile_expert_pair_project_s3_kernel(
             words = routed[:, 0:width].bitcast(F32).rearrange("p (u w) -> p u w", u=2)
             for n, b in enumerate(parts):
                 units["act", i, b] = words[:, :, 2 * P * n : 2 * P * (n + 1)]
+
+        def gate_quad(i):
+            staged[i] = work.tile([P, QUADS, K_PASS], BF16, name="staged", bufs=1, align_bytes=64)
+            first = (i - ON_VECTOR) * R_PASSES
+            for b in range(QUADS):
+                source = hr_quads[b][:, first : first + R_PASSES, :].rearrange("p g c -> p (g c)")
+                nc.vector.tensor_scalar(
+                    out=staged[i][:, b, :].rearrange("p (u w e) -> p w u e", u=2, e=2),
+                    in0=source.rearrange("p (w u e) -> p w u e", u=2, e=2),
+                    scalar1=gate_quads[:, b, i : i + 1],
+                    scalar2=None,
+                    op0=MULT,
+                )
+
+        def flip(i):
+            flipped[i] = work.tile([P, UNIT], F32, name="flipped", bufs=1, align_bytes=64)
+            words = staged[i][:].rearrange("p b k -> p (b k)").bitcast(F32)
+            nc.vector.transpose(out=flipped[i][:], in_=words)
+
+        def collect_flipped(i):
+            grouped["routed", i] = work.tile([P, ROUTED], BF16, name="grouped_r", bufs=2, align_bytes=256)
+            nc.scalar.copy(
+                out=grouped["routed", i][:].bitcast(F32).rearrange("p (g b r u) -> p g b r u", g=R_PASSES, b=QUADS, u=2),
+                in_=flipped[i][:].rearrange("p (b u g r) -> p g b r u", b=QUADS, u=2, g=R_PASSES),
+            )
 
         def order_hs(i, copy):
             ordered = work.tile([P, 2, 2 * P], F32, name="ordered", bufs=3)
@@ -144,10 +190,10 @@ def tile_expert_pair_project_s3_kernel(
         def collect(key, copy):
             if key[0] == "act" and key[2] < R_UNITS:
                 if key[2] == 0:
-                    grouped["routed", key[1]] = work.tile([P, ROUTED], BF16, name="grouped_r", bufs=3, align_bytes=256)
+                    grouped["routed", key[1]] = work.tile([P, ROUTED], BF16, name="grouped_r", bufs=2, align_bytes=256)
                 rows = grouped["routed", key[1]][:, key[2] * UNIT : (key[2] + 1) * UNIT]
             else:
-                single = work.tile([P, UNIT], BF16, name="grouped", bufs=3, align_bytes=256)
+                single = work.tile([P, UNIT], BF16, name="grouped", bufs=4, align_bytes=256)
                 rows = single[:]
             copy(
                 out=rows.bitcast(F32).rearrange("p (g r u) -> p g r u", g=2, u=2),
@@ -344,14 +390,14 @@ def tile_expert_pair_project_s3_kernel(
         load_resid(1)
         load_planes(wo_planes, wo_scales)
         nc.sync.dma_start(out=wo_sb[:], in_=wo_words.rearrange("g p n -> p g n"))
-        load_resid(2)
         load_hr(5)
-        load_resid(3)
-        load_hr(6)
+        load_resid(2)
         load_hs(3)
-        load_resid(4)
-        load_hr(7)
-        for i in range(5, TILES):
+        load_resid(3)
+        load_gate_quads()
+        for b in range(QUADS):
+            load_quads(b)
+        for i in range(4, TILES):
             load_resid(i)
 
         on_vector, on_scalar = nc.vector.tensor_copy, nc.scalar.copy
@@ -367,27 +413,25 @@ def tile_expert_pair_project_s3_kernel(
             for h in range(HALVES):
                 routed_pass(i, h, g)
 
-        twice = ident[:].unsqueeze(1).to_broadcast([P, 2, P])
+        def warm(copies, k):
+            bank = bank_tile(k, [P, copies, P])
+            moving = ident[:].unsqueeze(1).to_broadcast([P, copies, P])
+            nc.tensor.matmul(bank[:], lhsT=ident[:], rhs=moving, start=True, stop=True)
 
-        def warm(count, k):
-            bank = bank_tile(k, [P, BANK])
-            for n in range(count):
-                nc.tensor.matmul(bank[:, 0 : 2 * P], lhsT=ident[:], rhs=twice, start=True, stop=True)
-
-        warm(2, 7)
+        warm(4, 7)
         widen_on_vector(0, 0, 0)
         widen_on_scalar(0, 1, 0)
         widen_on_vector(0, 0, 1)
         apply_gate(0, (0,))
         turn(("act", 0, 0), 0)
-        warm(1, 7)
+        warm(2, 7)
         widen_on_scalar(0, 1, 1)
         widen_on_vector(0, 0, 2)
         collect(("act", 0, 0), on_scalar)
         widen_on_vector(0, 0, 3)
         apply_gate(0, (1,))
         turn(("act", 0, 1), 1)
-        warm(1, 7)
+        warm(2, 7)
         widen_on_scalar(0, 1, 2)
         interleave(0, 0, on_vector, slice(0, BANK // 2))
         apply_gate(1, (0,))
@@ -395,7 +439,7 @@ def tile_expert_pair_project_s3_kernel(
         collect(("act", 0, 1), on_scalar)
         turn(("act", 1, 0), 4)
         turn(("act", 1, 1), 5)
-        warm(1, 3)
+        warm(2, 3)
         widen_on_scalar(0, 1, 3)
         quantize(("act", 0, 0))
         apply_gate(2, (0,))
@@ -441,13 +485,13 @@ def tile_expert_pair_project_s3_kernel(
         collect(("act", 0, 2), on_scalar)
         collect(("act", 1, 2), on_scalar)
         widen_on_scalar(1, 1, 3)
+        order_hs(3, on_scalar)
         routed_both(0, 3)
         routed_both(1, 3)
         routed_both(2, 3)
         quantize_ws(0, 1)
         order_hs(2, on_vector)
         apply_gate(3, (0,))
-        order_hs(3, on_vector)
         quantize(("act", 0, 2))
         quantize_ws(1, 0)
         quantize(("act", 1, 2))
@@ -467,7 +511,7 @@ def tile_expert_pair_project_s3_kernel(
         quantize(("act", 2, 2))
         scale_pair(0, 0)
         quantize_ws(1, 1)
-        scale_pair(1, 0)
+        add_resid(0, (0,))
         turn(("act", 3, 1), 0)
         turn(("act", 3, 2), 1)
         collect(("act", 3, 1), on_scalar)
@@ -483,16 +527,16 @@ def tile_expert_pair_project_s3_kernel(
         scale_pair(0, 1)
         apply_gate(4)
         order_hs(4, on_scalar)
-        add_resid(0, (0,))
         add_resid(0, (1,))
+        scale_pair(1, 0)
         half_pair(3, 0, 2)
         turn(("act", 4, 0), 1)
-        turn(("z", 0), 0)
-        turn(("act", 4, 1), 4)
-        turn(("act", 4, 2), 3)
+        turn(("act", 4, 1), 0)
+        turn(("z", 0), 3)
+        turn(("act", 4, 2), 4)
         collect(("act", 4, 0), on_scalar)
-        collect(("z", 0), on_scalar)
         collect(("act", 4, 1), on_scalar)
+        collect(("z", 0), on_scalar)
         collect(("act", 4, 2), on_scalar)
         scale_pair(2, 0)
         scale_pair(1, 1)
@@ -504,14 +548,14 @@ def tile_expert_pair_project_s3_kernel(
         order_hs(5, on_scalar)
         project(0, 0, 5)
         project(0, 1, 7)
-        project(0, 2, 0)
+        project(0, 2, 3)
         store(0)
         quantize(("act", 4, 2))
         add_resid(1)
         apply_gate(5)
 
         taken = []
-        ring = (1, 4, 3, 2, 5, 7, 0, 6)
+        ring = (1, 0, 4, 2, 5, 7, 3, 6)
 
         def next_bank():
             taken.append(ring[len(taken) % BANKS])
@@ -522,29 +566,68 @@ def tile_expert_pair_project_s3_kernel(
             collect(key, on_scalar)
 
         last = TILES - 1
-        for i in range(OPENING + 1, last):
-            half_pair(i, 0, next_bank())
-            scale_pair(i - 1, 1)
-            turn_next(("z", i - LAG))
-            for b in range(3):
-                turn_next(("act", i + 1, b))
-            scale_pair(i, 0)
-            quantize(("z", i - LAG))
-            add_resid(i - 2 if i == OPENING + 1 else i - 1)
-            quantize_routed(i + 1)
-            half_pair(i, 1, next_bank())
-            quantize(("act", i + 1, R_UNITS))
-            if i + 2 < TILES:
-                order_hs(i + 2, on_scalar)
-            for n in range(OUT_BANKS):
-                project(i - LAG, n, next_bank())
-            store(i - LAG)
-            if i + 2 < TILES:
-                apply_gate(i + 2)
-            if i == OPENING + 1:
-                add_resid(i - 1)
-            if i == last - 1:
-                add_resid(i, (0,))
+        half_pair(4, 0, next_bank())
+        scale_pair(3, 1)
+        add_resid(2)
+        turn(("z", 1), next_bank())
+        turn(("act", 5, 0), next_bank())
+        turn(("act", 5, 1), next_bank())
+        turn(("act", 5, 2), next_bank())
+        collect(("z", 1), on_scalar)
+        collect(("act", 5, 0), on_scalar)
+        collect(("act", 5, 1), on_scalar)
+        collect(("act", 5, 2), on_scalar)
+        scale_pair(4, 0)
+        quantize(("z", 1))
+        half_pair(4, 1, next_bank())
+        quantize_routed(5)
+        quantize(("act", 5, 2))
+        add_resid(3)
+        order_hs(6, on_scalar)
+        order_hs(7, on_scalar)
+        project(1, 0, next_bank())
+        project(1, 1, next_bank())
+        project(1, 2, next_bank())
+        store(1)
+        gate_quad(6)
+        scale_pair(4, 1)
+        flip(6)
+        half_pair(5, 0, next_bank())
+        collect_flipped(6)
+        gate_quad(7)
+        turn(("z", 2), next_bank())
+        turn(("act", 6, 2), next_bank())
+        turn(("act", 7, 2), next_bank())
+        turn(("z", 3), next_bank())
+        collect(("z", 2), on_scalar)
+        collect(("act", 6, 2), on_scalar)
+        collect(("act", 7, 2), on_scalar)
+        collect(("z", 3), on_scalar)
+        scale_pair(5, 0)
+        quantize_routed(6)
+        quantize(("z", 2))
+        add_resid(4)
+        half_pair(5, 1, next_bank())
+        quantize(("act", 6, 2))
+        flip(7)
+        project(2, 0, next_bank())
+        project(2, 1, next_bank())
+        project(2, 2, next_bank())
+        store(2)
+        scale_pair(5, 1)
+        collect_flipped(7)
+        half_pair(6, 0, next_bank())
+        quantize(("z", 3))
+        quantize(("act", 7, 2))
+        add_resid(5)
+        scale_pair(6, 0)
+        half_pair(6, 1, next_bank())
+        quantize_routed(7)
+        project(3, 0, next_bank())
+        project(3, 1, next_bank())
+        project(3, 2, next_bank())
+        store(3)
+        add_resid(6, (0,))
 
         half_pair(last, 0, next_bank())
         scale_pair(last - 1, 1)

@@ -36,6 +36,7 @@ OPENING = 3
 QUAD = 32
 QUADS = P // QUAD
 ON_VECTOR = 6
+GATED_ON_SCALAR = 2
 LAG = 3
 
 
@@ -55,6 +56,7 @@ def tile_expert_pair_project_s3_kernel(
         out_rows = out.rearrange("(p i) n -> p i n", i=TILES)
 
         gate_sb = keep.tile([P, TILES], BF16, name="gate_sb")
+        gate_f32 = keep.tile([P, TILES], F32, name="gate_f32")
         gain_sb = keep.tile([P, CHANNELS], BF16, name="gain_sb")
         hs_pairs = [keep.tile([P, 2, SHARED], BF16, name="hs%d" % j) for j in range(TILES // 2)]
         hs_sb = [hs_pairs[i // 2][:, i % 2, :] for i in range(TILES)]
@@ -62,6 +64,7 @@ def tile_expert_pair_project_s3_kernel(
         late = TILES - ON_VECTOR
         hr_quads = [keep.tile([P, late * R_PASSES, P], BF16, name="hr_quad%d" % b) for b in range(QUADS)]
         gate_quads = keep.tile([P, QUADS, TILES], BF16, name="gate_quads")
+        gate_wide = keep.tile([P, QUADS, TILES], F32, name="gate_wide")
         staged = {}
         flipped = {}
         resid_sb = [keep.tile([P, CHANNELS], BF16, name="resid%d" % i) for i in range(TILES)]
@@ -147,18 +150,18 @@ def tile_expert_pair_project_s3_kernel(
             for n, b in enumerate(parts):
                 units["act", i, b] = words[:, :, 2 * P * n : 2 * P * (n + 1)]
 
-        def gate_quad(i):
-            staged[i] = work.tile([P, QUADS, K_PASS], BF16, name="staged", bufs=1, align_bytes=64)
+        def gate_quad(i, groups):
+            if i not in staged:
+                staged[i] = work.tile([P, QUADS, K_PASS], BF16, name="staged", bufs=2, align_bytes=64)
             first = (i - ON_VECTOR) * R_PASSES
-            for b in range(QUADS):
-                source = hr_quads[b][:, first : first + R_PASSES, :].rearrange("p g c -> p (g c)")
-                nc.vector.tensor_scalar(
-                    out=staged[i][:, b, :].rearrange("p (u w e) -> p w u e", u=2, e=2),
-                    in0=source.rearrange("p (w u e) -> p w u e", u=2, e=2),
-                    scalar1=gate_quads[:, b, i : i + 1],
-                    scalar2=None,
-                    op0=MULT,
-                )
+            for b in groups:
+                source = hr_quads[b][:, first : first + R_PASSES, :].rearrange("p g (w u e) -> p (g w) u e", u=2, e=2)
+                target = staged[i][:, b, :].rearrange("p (u w e) -> p w u e", u=2, e=2)
+                factor = gate_wide[:, b, i : i + 1]
+                if b < GATED_ON_SCALAR:
+                    nc.scalar.activation(out=target, in_=source, func=COPY, scale=factor)
+                else:
+                    nc.vector.tensor_scalar(out=target, in0=source, scalar1=factor, scalar2=None, op0=MULT)
 
         def flip(i):
             flipped[i] = work.tile([P, UNIT], F32, name="flipped", bufs=1, align_bytes=64)
@@ -171,6 +174,16 @@ def tile_expert_pair_project_s3_kernel(
                 out=grouped["routed", i][:].bitcast(F32).rearrange("p (g b r u) -> p g b r u", g=R_PASSES, b=QUADS, u=2),
                 in_=flipped[i][:].rearrange("p (b u g r) -> p g b r u", b=QUADS, u=2, g=R_PASSES),
             )
+
+        def gate_on_scalar(i, b):
+            routed = work.tile([P, ROUTED], BF16, name="routed", bufs=2)
+            nc.scalar.activation(
+                out=routed[:, 0:UNIT].rearrange("p (u w e) -> p w u e", u=2, e=2),
+                in_=hr_sb[i][:, b * UNIT : (b + 1) * UNIT].rearrange("p (w u e) -> p w u e", u=2, e=2),
+                func=COPY,
+                scale=gate_f32[:, i : i + 1],
+            )
+            units["act", i, b] = routed[:, 0:UNIT].bitcast(F32).rearrange("p (u w) -> p u w", u=2)
 
         def order_hs(i, copy):
             ordered = work.tile([P, 2, 2 * P], F32, name="ordered", bufs=3)
@@ -206,6 +219,25 @@ def tile_expert_pair_project_s3_kernel(
             planes = work.tile([P, 2 * P], U8, name="planes", bufs=8, align_bytes=256)
             nc.vector.quantize_mx(out=codes[:].bitcast(FP8X4), scales=planes[:], in_=grouped[key])
             operands[key] = (codes[:], planes[:])
+
+        def turn_pass(key, g, k):
+            bank = bank_tile(k, [P, 2, P])
+            for u in range(2):
+                nc.tensor.transpose(bank[:, u, :], units[key][:, u, g * P : (g + 1) * P], ident[:])
+            turned[key, g] = bank
+
+        def collect_pass(key, g, copy):
+            rows = work.tile([P, K_PASS], BF16, name="grouped_pass", bufs=2, align_bytes=256)
+            copy(out=rows[:].bitcast(F32).rearrange("p (r u) -> p r u", u=2), in_=turned[key, g][:].rearrange("p u r -> p r u"))
+            grouped[key, g] = rows
+
+        def quantize_pass(key, g):
+            if g == 0:
+                codes = work.tile([P, 2 * P], U32, name="codes", bufs=8, align_bytes=256)
+                planes = work.tile([P, 2 * P], U8, name="planes", bufs=8, align_bytes=256)
+                operands[key] = (codes[:], planes[:])
+            codes, planes = stationary(key, g)
+            nc.vector.quantize_mx(out=codes, scales=planes, in_=grouped[key, g][:])
 
         def quantize_routed(i):
             codes = work.tile([P, 4 * P], U32, name="codes_r", bufs=4, align_bytes=256)
@@ -304,9 +336,45 @@ def tile_expert_pair_project_s3_kernel(
             for g in range(S_PASSES):
                 shared_pass(i, h, g)
 
+        def quarter_pair(i, cols, k):
+            bank = bank_tile(k, [P, cols.stop - cols.start])
+            h, inside = cols.start // BANK, slice(cols.start % BANK, (cols.stop - 1) % BANK + 1)
+            for g in range(R_PASSES + S_PASSES):
+                codes, planes = stationary(("act", i, g // 2), g % 2)
+                if g < R_PASSES:
+                    rhs = wr_sb[g][:, 2 * cols.start : 2 * cols.stop].bitcast(FP4X4)
+                    rhs_scale = wr_planes[g // 2][:, g % 2, cols.start // 4 : cols.stop // 4].bitcast(U8)
+                else:
+                    rhs = ws_codes[g - R_PASSES, h][:, inside].bitcast(FP8X4)
+                    rhs_scale = ws_planes[g - R_PASSES, h][:, inside]
+                nc.tensor.matmul_mx(
+                    out=bank[:],
+                    lhsT=codes,
+                    lhsT_scale=planes,
+                    rhs=rhs,
+                    rhs_scale=rhs_scale,
+                    start=(g == 0),
+                    stop=(g == R_PASSES + S_PASSES - 1),
+                )
+            pair_banks[i, cols.start] = bank
+
+        def scale_quarter(i, cols):
+            nc.vector.tensor_tensor(
+                out=scaled_pairs[i][:, cols], in0=pair_banks[i, cols.start][:], in1=gain_sb[:, cols], op=MULT
+            )
+
+        def add_quarter(i, cols):
+            words = slice(cols.start // PACK, cols.stop // PACK)
+            nc.vector.tensor_tensor(
+                out=z_rows[i][:].rearrange("p (u w e) -> p u w e", u=2, e=2)[:, :, words, :],
+                in0=split(scaled_pairs[i][:, cols]),
+                in1=split(resid_sb[i][:, cols]),
+                op=ADD,
+            )
+
         def scale_pair(i, h):
             if (i, 1 - h) not in scaled_pairs:
-                scaled_pairs[i] = work.tile([P, CHANNELS], F32, name="scaled", bufs=4)
+                scaled_pairs[i] = work.tile([P, CHANNELS], F32, name="scaled", bufs=3)
             scaled_pairs[i, h] = True
             channels = slice(h * BANK, (h + 1) * BANK)
             nc.vector.tensor_tensor(
@@ -315,7 +383,7 @@ def tile_expert_pair_project_s3_kernel(
 
         def add_resid(i, halves=(0, 1)):
             if halves[0] == 0:
-                z_rows[i] = work.tile([P, UNIT], BF16, name="z", bufs=5)
+                z_rows[i] = work.tile([P, UNIT], BF16, name="z", bufs=4)
                 units["z", i] = z_rows[i][:].bitcast(F32).rearrange("p (u w) -> p u w", u=2)
             channels = slice(halves[0] * BANK, (halves[-1] + 1) * BANK)
             words = slice(halves[0] * P, (halves[-1] + 1) * P)
@@ -426,6 +494,7 @@ def tile_expert_pair_project_s3_kernel(
         turn(("act", 0, 0), 0)
         warm(2, 7)
         widen_on_scalar(0, 1, 1)
+        nc.scalar.copy(out=gate_f32[:], in_=gate_sb[:])
         widen_on_vector(0, 0, 2)
         collect(("act", 0, 0), on_scalar)
         widen_on_vector(0, 0, 3)
@@ -511,7 +580,7 @@ def tile_expert_pair_project_s3_kernel(
         quantize(("act", 2, 2))
         scale_pair(0, 0)
         quantize_ws(1, 1)
-        add_resid(0, (0,))
+        scale_pair(1, 0)
         turn(("act", 3, 1), 0)
         turn(("act", 3, 2), 1)
         collect(("act", 3, 1), on_scalar)
@@ -522,23 +591,23 @@ def tile_expert_pair_project_s3_kernel(
         shared_pass(0, 1, 1)
         shared_pass(1, 1, 1)
         shared_pass(2, 1, 1)
+        gate_on_scalar(4, 1)
+        order_hs(4, on_scalar)
         quantize_routed(3)
         quantize(("act", 3, 2))
         scale_pair(0, 1)
-        apply_gate(4)
-        order_hs(4, on_scalar)
-        add_resid(0, (1,))
-        scale_pair(1, 0)
+        apply_gate(4, (0,))
+        add_resid(0)
+        scale_pair(2, 0)
         half_pair(3, 0, 2)
         turn(("act", 4, 0), 1)
         turn(("act", 4, 1), 0)
-        turn(("z", 0), 3)
         turn(("act", 4, 2), 4)
+        turn(("z", 0), 3)
         collect(("act", 4, 0), on_scalar)
-        collect(("act", 4, 1), on_scalar)
         collect(("z", 0), on_scalar)
+        collect(("act", 4, 1), on_scalar)
         collect(("act", 4, 2), on_scalar)
-        scale_pair(2, 0)
         scale_pair(1, 1)
         scale_pair(2, 1)
         quantize(("z", 0))
@@ -569,6 +638,7 @@ def tile_expert_pair_project_s3_kernel(
         half_pair(4, 0, next_bank())
         scale_pair(3, 1)
         add_resid(2)
+        nc.scalar.copy(out=gate_wide[:], in_=gate_quads[:])
         turn(("z", 1), next_bank())
         turn(("act", 5, 0), next_bank())
         turn(("act", 5, 1), next_bank())
@@ -582,71 +652,95 @@ def tile_expert_pair_project_s3_kernel(
         half_pair(4, 1, next_bank())
         quantize_routed(5)
         quantize(("act", 5, 2))
-        add_resid(3)
         order_hs(6, on_scalar)
         order_hs(7, on_scalar)
+        scale_pair(4, 1)
+        add_resid(3)
         project(1, 0, next_bank())
+        gate_quad(6, range(GATED_ON_SCALAR))
+        gate_quad(6, range(GATED_ON_SCALAR, QUADS))
         project(1, 1, next_bank())
         project(1, 2, next_bank())
         store(1)
-        gate_quad(6)
-        scale_pair(4, 1)
         flip(6)
         half_pair(5, 0, next_bank())
-        collect_flipped(6)
-        gate_quad(7)
+        gate_quad(7, range(GATED_ON_SCALAR, QUADS))
         turn(("z", 2), next_bank())
         turn(("act", 6, 2), next_bank())
         turn(("act", 7, 2), next_bank())
         turn(("z", 3), next_bank())
         collect(("z", 2), on_scalar)
+        collect_flipped(6)
         collect(("act", 6, 2), on_scalar)
-        collect(("act", 7, 2), on_scalar)
-        collect(("z", 3), on_scalar)
         scale_pair(5, 0)
-        quantize_routed(6)
         quantize(("z", 2))
         add_resid(4)
         half_pair(5, 1, next_bank())
+        gate_quad(7, range(GATED_ON_SCALAR))
+        quantize_routed(6)
         quantize(("act", 6, 2))
-        flip(7)
+        collect(("act", 7, 2), on_scalar)
+        collect(("z", 3), on_scalar)
         project(2, 0, next_bank())
         project(2, 1, next_bank())
         project(2, 2, next_bank())
         store(2)
         scale_pair(5, 1)
-        collect_flipped(7)
+        flip(7)
         half_pair(6, 0, next_bank())
+        collect_flipped(7)
         quantize(("z", 3))
-        quantize(("act", 7, 2))
         add_resid(5)
         scale_pair(6, 0)
         half_pair(6, 1, next_bank())
         quantize_routed(7)
+        quantize(("act", 7, 2))
+        scale_pair(6, 1)
         project(3, 0, next_bank())
         project(3, 1, next_bank())
         project(3, 2, next_bank())
         store(3)
-        add_resid(6, (0,))
 
-        half_pair(last, 0, next_bank())
-        scale_pair(last - 1, 1)
-        add_resid(last - 1, (1,))
-        for j in range(last - LAG, last):
+        def banks_of(i):
+            return [slice(n * BANK, (n + 1) * BANK) for n in range(OUT_BANKS)]
+
+        def project_and_store(i, cols, copy):
+            project_pass(i, cols, 0, next_bank())
+            project_pass(i, cols, 1)
+            empty(i, cols, copy)
+            store(i, cols)
+
+        head, middle, end = banks_of(last)
+        for j in (last - 3, last - 2):
             turn_next(("z", j))
-        scale_pair(last, 0)
-        half_pair(last, 1, next_bank())
+        half_pair(last, 0, next_bank())
+        add_resid(last - 1)
         quantize(("z", last - 3))
-        add_resid(last, (0,))
         quantize(("z", last - 2))
-        scale_pair(last, 1)
+        scale_pair(last, 0)
+        for cols in (head, middle, end):
+            project_and_store(last - 3, cols, on_scalar)
+        add_resid(last, (0,))
+        turn(("z", last - 1), next_bank())
+        collect(("z", last - 1), on_vector)
+        project_and_store(last - 2, head, on_scalar)
         quantize(("z", last - 1))
-        add_resid(last, (1,))
-        for i in range(last - LAG, TILES):
-            if i == last - 1:
-                turn(("z", last), next_bank())
-                collect(("z", last), on_vector)
-                quantize(("z", last))
-            for n in range(OUT_BANKS):
-                project(i, n, next_bank(), on_vector if i > last - LAG and n == 1 else on_scalar)
-                store(i, slice(n * BANK, (n + 1) * BANK))
+        quarters = (slice(BANK, BANK + BANK // 2), slice(BANK + BANK // 2, CHANNELS))
+        for cols in quarters:
+            quarter_pair(last, cols, next_bank())
+            scale_quarter(last, cols)
+            add_quarter(last, cols)
+        project_and_store(last - 2, middle, on_scalar)
+        project_and_store(last - 2, end, on_vector)
+        project_and_store(last - 1, head, on_scalar)
+        for g in range(HALVES):
+            turn_pass(("z", last), g, next_bank())
+        collect_pass(("z", last), 0, on_vector)
+        collect_pass(("z", last), 1, on_scalar)
+        for g in range(HALVES):
+            quantize_pass(("z", last), g)
+        project_and_store(last - 1, middle, on_scalar)
+        project_and_store(last - 1, end, on_vector)
+        project_and_store(last, head, on_scalar)
+        project_and_store(last, middle, on_vector)
+        project_and_store(last, end, on_scalar)

@@ -37,6 +37,7 @@ QUAD = 32
 QUADS = P // QUAD
 ON_VECTOR = 6
 GATED_ON_SCALAR = 2
+SHIFT = 128
 LAG = 3
 
 
@@ -70,10 +71,12 @@ def tile_expert_pair_project_s3_kernel(
         resid_sb = [keep.tile([P, CHANNELS], BF16, name="resid%d" % i) for i in range(TILES)]
         wr_sb = [keep.tile([P, 2 * CHANNELS], U8, name="wr%d" % g, align_bytes=256) for g in range(R_PASSES)]
         wo_sb = keep.tile([P, HALVES, 2 * FEATURES], U8, name="wo_sb", align_bytes=256)
-        wr_planes = [
-            keep.tile([P, 2, CHANNELS // 4], I32, name="wr_planes%d" % b, align_bytes=256) for b in range(R_UNITS)
-        ]
-        wo_planes = keep.tile([P, HALVES, FEATURES // 4], I32, name="wo_planes", align_bytes=256)
+        def shifted(name, rows, width):
+            whole = keep.tile([P, SHIFT // 4 + rows * width // 4], I32, name=name, align_bytes=256)
+            return whole[:, SHIFT // 4 :].rearrange("p (g n) -> p g n", g=rows)
+
+        wr_planes = [shifted("wr_planes%d" % b, 2, CHANNELS) for b in range(R_UNITS)]
+        wo_planes = shifted("wo_planes", HALVES, FEATURES)
         ws_scale_sb = keep.tile([P, S_PASSES, PACK], F32, name="ws_scale_sb")
         ws_raw = [
             [keep.tile([P, 2, CHANNELS], U8, name="ws_raw%d%d" % (g, j)) for j in range(2)] for g in range(S_PASSES)
@@ -82,7 +85,9 @@ def tile_expert_pair_project_s3_kernel(
         ws_parts = [(g, h) for g in range(S_PASSES) for h in range(HALVES)]
         ws_wide = {gh: keep.tile([P, PACK, BANK], BF16, name="ws_wide%d%d" % gh) for gh in ws_parts}
         ws_codes = {gh: keep.tile([P, BANK], U32, name="ws_codes%d%d" % gh, align_bytes=256) for gh in ws_parts}
-        ws_planes = {gh: keep.tile([P, BANK], U8, name="ws_planes%d%d" % gh, align_bytes=256) for gh in ws_parts}
+        ws_planes = {
+            gh: keep.tile([P, SHIFT + BANK], U8, name="ws_planes%d%d" % gh, align_bytes=256)[:, SHIFT:] for gh in ws_parts
+        }
         ws_packed = {}
 
         ident = keep.tile([P, P], F32, name="ident")

@@ -58,28 +58,28 @@ def tile_expert_pair_project_s3_kernel(
 
         gate_sb = keep.tile([P, TILES], BF16, name="gate_sb")
         gate_f32 = keep.tile([P, TILES], F32, name="gate_f32")
-        gain_sb = keep.tile([P, CHANNELS], BF16, name="gain_sb")
-        hs_pairs = [keep.tile([P, 2, SHARED], BF16, name="hs%d" % j) for j in range(TILES // 2)]
+        gain_sb = keep.tile([P, CHANNELS], BF16, name="gain_sb", align_bytes=256)
+        hs_pairs = [keep.tile([P, 2, SHARED], BF16, name="hs%d" % j, align_bytes=256) for j in range(TILES // 2)]
         hs_sb = [hs_pairs[i // 2][:, i % 2, :] for i in range(TILES)]
-        hr_sb = [keep.tile([P, ROUTED], BF16, name="hr%d" % i) for i in range(ON_VECTOR)]
+        hr_sb = [keep.tile([P, ROUTED], BF16, name="hr%d" % i, align_bytes=256) for i in range(ON_VECTOR)]
         late = TILES - ON_VECTOR
-        hr_quads = [keep.tile([P, late * R_PASSES, P], BF16, name="hr_quad%d" % b) for b in range(QUADS)]
+        hr_quads = [keep.tile([P, late * R_PASSES, P], BF16, name="hr_quad%d" % b, align_bytes=256) for b in range(QUADS)]
         gate_quads = keep.tile([P, QUADS, TILES], BF16, name="gate_quads")
         gate_wide = keep.tile([P, QUADS, TILES], F32, name="gate_wide")
         staged = {}
         flipped = {}
-        resid_sb = [keep.tile([P, CHANNELS], BF16, name="resid%d" % i) for i in range(TILES)]
+        resid_sb = [keep.tile([P, CHANNELS], BF16, name="resid%d" % i, align_bytes=256) for i in range(TILES)]
         wr_sb = [keep.tile([P, 2 * CHANNELS], U8, name="wr%d" % g, align_bytes=256) for g in range(R_PASSES)]
         wo_sb = keep.tile([P, HALVES, 2 * FEATURES], U8, name="wo_sb", align_bytes=256)
         def shifted(name, rows, width):
-            whole = keep.tile([P, SHIFT // 4 + rows * width // 4], I32, name=name, align_bytes=256)
-            return whole[:, SHIFT // 4 :].rearrange("p (g n) -> p g n", g=rows)
+            whole = keep.tile([P, rows * width // 4], I32, name=name, align_bytes=256)
+            return whole[:].rearrange("p (g n) -> p g n", g=rows)
 
         wr_planes = [shifted("wr_planes%d" % b, 2, CHANNELS) for b in range(R_UNITS)]
         wo_planes = shifted("wo_planes", HALVES, FEATURES)
         ws_scale_sb = keep.tile([P, S_PASSES, PACK], F32, name="ws_scale_sb")
         ws_raw = [
-            [keep.tile([P, 2, CHANNELS], U8, name="ws_raw%d%d" % (g, j)) for j in range(2)] for g in range(S_PASSES)
+            [keep.tile([P, 2, CHANNELS], U8, name="ws_raw%d%d" % (g, j), align_bytes=256) for j in range(2)] for g in range(S_PASSES)
         ]
 
         ws_parts = [(g, h) for g in range(S_PASSES) for h in range(HALVES)]
@@ -157,7 +157,7 @@ def tile_expert_pair_project_s3_kernel(
 
         def gate_quad(i, groups):
             if i not in staged:
-                staged[i] = work.tile([P, QUADS, K_PASS], BF16, name="staged", bufs=2, align_bytes=64)
+                staged[i] = work.tile([P, QUADS, K_PASS], BF16, name="staged", bufs=1, align_bytes=64)
             first = (i - ON_VECTOR) * R_PASSES
             for b in groups:
                 source = hr_quads[b][:, first : first + R_PASSES, :].rearrange("p g (w u e) -> p (g w) u e", u=2, e=2)
@@ -245,8 +245,8 @@ def tile_expert_pair_project_s3_kernel(
             nc.vector.quantize_mx(out=codes, scales=planes, in_=grouped[key, g][:])
 
         def quantize_routed(i):
-            codes = work.tile([P, 4 * P], U32, name="codes_r", bufs=4, align_bytes=256)
-            planes = work.tile([P, 4 * P], U8, name="planes_r", bufs=4, align_bytes=256)
+            codes = work.tile([P, 4 * P], U32, name="codes_r", bufs=3, align_bytes=256)
+            planes = work.tile([P, 4 * P], U8, name="planes_r", bufs=3, align_bytes=256)
             nc.vector.quantize_mx(out=codes[:].bitcast(FP8X4), scales=planes[:], in_=grouped["routed", i][:])
             for b in range(R_UNITS):
                 cols = slice(2 * P * b, 2 * P * (b + 1))
@@ -415,7 +415,7 @@ def tile_expert_pair_project_s3_kernel(
 
         def empty(i, cols, copy):
             if cols.start == 0:
-                results[i] = work.tile([P, FEATURES], F32, name="result", bufs=3)
+                results[i] = work.tile([P, FEATURES], F32, name="result", bufs=3, align_bytes=256)
             copy(out=results[i][:, cols], in_=out_banks[i, cols.start][:])
 
         def project(i, n, k, copy=nc.scalar.copy):

@@ -37,7 +37,6 @@ QUAD = 32
 QUADS = P // QUAD
 ON_VECTOR = 6
 GATED_ON_SCALAR = 2
-SHIFT = 128
 LAG = 3
 
 
@@ -86,7 +85,7 @@ def tile_expert_pair_project_s3_kernel(
         ws_wide = {gh: keep.tile([P, PACK, BANK], BF16, name="ws_wide%d%d" % gh) for gh in ws_parts}
         ws_codes = {gh: keep.tile([P, BANK], U32, name="ws_codes%d%d" % gh, align_bytes=256) for gh in ws_parts}
         ws_planes = {
-            gh: keep.tile([P, SHIFT + BANK], U8, name="ws_planes%d%d" % gh, align_bytes=256)[:, SHIFT:] for gh in ws_parts
+            gh: keep.tile([P, BANK], U8, name="ws_planes%d%d" % gh, align_bytes=256)[:] for gh in ws_parts
         }
         ws_packed = {}
 
@@ -245,8 +244,8 @@ def tile_expert_pair_project_s3_kernel(
             nc.vector.quantize_mx(out=codes, scales=planes, in_=grouped[key, g][:])
 
         def quantize_routed(i):
-            codes = work.tile([P, 4 * P], U32, name="codes_r", bufs=3, align_bytes=256)
-            planes = work.tile([P, 4 * P], U8, name="planes_r", bufs=3, align_bytes=256)
+            codes = work.tile([P, 4 * P], U32, name="codes_r", bufs=4, align_bytes=256)
+            planes = work.tile([P, 4 * P], U8, name="planes_r", bufs=4, align_bytes=256)
             nc.vector.quantize_mx(out=codes[:].bitcast(FP8X4), scales=planes[:], in_=grouped["routed", i][:])
             for b in range(R_UNITS):
                 cols = slice(2 * P * b, 2 * P * (b + 1))
@@ -669,7 +668,6 @@ def tile_expert_pair_project_s3_kernel(
         store(1)
         flip(6)
         half_pair(5, 0, next_bank())
-        gate_quad(7, range(GATED_ON_SCALAR, QUADS))
         turn(("z", 2), next_bank())
         turn(("act", 6, 2), next_bank())
         turn(("act", 7, 2), next_bank())
@@ -690,6 +688,7 @@ def tile_expert_pair_project_s3_kernel(
         project(2, 1, next_bank())
         project(2, 2, next_bank())
         store(2)
+        gate_quad(7, range(GATED_ON_SCALAR, QUADS))
         scale_pair(5, 1)
         flip(7)
         half_pair(6, 0, next_bank())

@@ -141,7 +141,7 @@ def tile_expert_pair_project_s3_kernel(
 
         def apply_gate(i, parts=(0, 1)):
             width = len(parts) * UNIT
-            routed = work.tile([P, ROUTED], BF16, name="routed", bufs=2)
+            routed = work.tile([P, width], BF16, name="routed%d" % len(parts), bufs=2 if len(parts) == 1 else 1)
             source = hr_sb[i][:, parts[0] * UNIT : parts[0] * UNIT + width]
             nc.vector.tensor_scalar(
                 out=routed[:, 0:width].rearrange("p (u w e) -> p w u e", u=2, e=2),
@@ -180,7 +180,7 @@ def tile_expert_pair_project_s3_kernel(
             )
 
         def gate_on_scalar(i, b):
-            routed = work.tile([P, ROUTED], BF16, name="routed", bufs=2)
+            routed = work.tile([P, UNIT], BF16, name="routed1", bufs=2)
             nc.scalar.activation(
                 out=routed[:, 0:UNIT].rearrange("p (u w e) -> p w u e", u=2, e=2),
                 in_=hr_sb[i][:, b * UNIT : (b + 1) * UNIT].rearrange("p (w u e) -> p w u e", u=2, e=2),
@@ -205,7 +205,7 @@ def tile_expert_pair_project_s3_kernel(
             turned[key] = bank
 
         def collect(key, copy):
-            if key[0] == "act" and key[2] < R_UNITS:
+            if key[0] == "act" and key[2] < R_UNITS and key[1] > OPENING:
                 if key[2] == 0:
                     grouped["routed", key[1]] = work.tile([P, ROUTED], BF16, name="grouped_r", bufs=2, align_bytes=256)
                 rows = grouped["routed", key[1]][:, key[2] * UNIT : (key[2] + 1) * UNIT]
@@ -433,11 +433,55 @@ def tile_expert_pair_project_s3_kernel(
         nc.vector.memset(wo_planes[:], 0)
         make_identity(nc, ident[:])
         nc.scalar.activation(out=primer[:, 1:2], in_=primer[:, 0:1], func=COPY)
-
         first, second = slice(0, UNIT), slice(UNIT, ROUTED)
-        nc.sync.dma_start(out=ws_scale_sb[:], in_=ws_scale.rearrange("(g p t) o -> p g (t o)", p=P, t=PACK))
+        on_vector, on_scalar = nc.vector.tensor_copy, nc.scalar.copy
+
+        def load_small():
+            nc.sync.dma_start(out=gate_sb[:], in_=gate.rearrange("(p i) -> p i", i=TILES))
+
+        def load_scale():
+            nc.sync.dma_start(out=ws_scale_sb[:], in_=ws_scale.rearrange("(g p t) o -> p g (t o)", p=P, t=PACK))
+
+        def load_gain():
+            nc.sync.dma_start(out=gain_sb[:], in_=gain.partition_broadcast(P))
+
+        def load_wo():
+            load_planes(wo_planes, wo_scales)
+            nc.sync.dma_start(out=wo_sb[:], in_=wo_words.rearrange("g p n -> p g n"))
+
+        def routed_both(i, g):
+            for h in range(HALVES):
+                routed_pass(i, h, g)
+
+        def routed_half(i, h):
+            for g in range(R_PASSES):
+                routed_pass(i, h, g)
+
+        def shared_half(i, h):
+            for g in range(S_PASSES):
+                shared_pass(i, h, g)
+
+        def open_tile(i, k0, k1):
+            open_pair(i, 0, k0)
+            open_pair(i, 1, k1)
+
+        def warm(copies, k):
+            bank = bank_tile(k, [P, copies, P])
+            moving = ident[:].unsqueeze(1).to_broadcast([P, copies, P])
+            nc.tensor.matmul(bank[:], lhsT=ident[:], rhs=moving, start=True, stop=True)
+
+        def banks_of(i):
+            return [slice(n * BANK, (n + 1) * BANK) for n in range(OUT_BANKS)]
+
+        def project_and_store(i, cols, copy, k):
+            project_pass(i, cols, 0, k)
+            project_pass(i, cols, 1)
+            empty(i, cols, copy)
+            store(i, cols)
+
+        load_scale()
         load_ws(0, 0)
-        nc.sync.dma_start(out=gate_sb[:], in_=gate.rearrange("(p i) -> p i", i=TILES))
+        load_small()
         load_hr(0, first)
         load_ws(0, 1)
         load_hr(0, second)
@@ -455,41 +499,25 @@ def tile_expert_pair_project_s3_kernel(
         load_hs(1)
         load_hr(3, first)
         load_hr(3, second)
-        nc.sync.dma_start(out=gain_sb[:], in_=gain.partition_broadcast(P))
+        load_gain()
         load_resid(0)
         load_hr(4)
         load_hs(2)
         load_resid(1)
-        load_planes(wo_planes, wo_scales)
-        nc.sync.dma_start(out=wo_sb[:], in_=wo_words.rearrange("g p n -> p g n"))
+        load_wo()
         load_hr(5)
         load_resid(2)
         load_hs(3)
         load_resid(3)
         load_gate_quads()
-        for b in range(QUADS):
-            load_quads(b)
-        for i in range(4, TILES):
-            load_resid(i)
-
-        on_vector, on_scalar = nc.vector.tensor_copy, nc.scalar.copy
-        for i in range(OPENING + 1):
-            units["act", i, R_UNITS] = hs_sb[i].bitcast(F32).rearrange("p (w u) -> p u w", u=2)
-        pair_places = ((2, 3), (4, 5), (6, 7))
-
-        def open_tile(i):
-            for h in range(HALVES):
-                open_pair(i, h, pair_places[i][h])
-
-        def routed_both(i, g):
-            for h in range(HALVES):
-                routed_pass(i, h, g)
-
-        def warm(copies, k):
-            bank = bank_tile(k, [P, copies, P])
-            moving = ident[:].unsqueeze(1).to_broadcast([P, copies, P])
-            nc.tensor.matmul(bank[:], lhsT=ident[:], rhs=moving, start=True, stop=True)
-
+        load_quads(0)
+        load_quads(1)
+        load_quads(2)
+        load_quads(3)
+        load_resid(4)
+        load_resid(5)
+        load_resid(6)
+        load_resid(7)
         warm(4, 7)
         widen_on_vector(0, 0, 0)
         widen_on_scalar(0, 1, 0)
@@ -506,7 +534,7 @@ def tile_expert_pair_project_s3_kernel(
         turn(("act", 0, 1), 1)
         warm(2, 7)
         widen_on_scalar(0, 1, 2)
-        interleave(0, 0, on_vector, slice(0, BANK // 2))
+        interleave(0, 0, on_vector, slice(0, 256))
         apply_gate(1, (0,))
         apply_gate(1, (1,))
         collect(("act", 0, 1), on_scalar)
@@ -525,15 +553,15 @@ def tile_expert_pair_project_s3_kernel(
         quantize(("act", 1, 0))
         collect(("act", 2, 0), on_scalar)
         collect(("act", 2, 1), on_scalar)
-        interleave(0, 0, on_vector, slice(BANK // 2, BANK))
-        open_tile(0)
+        interleave(0, 0, on_vector, slice(256, 512))
+        open_tile(0, 2, 3)
         routed_both(0, 0)
         routed_both(0, 1)
-        open_tile(1)
+        open_tile(1, 4, 5)
         routed_both(1, 0)
         routed_both(1, 1)
         quantize(("act", 2, 0))
-        open_tile(2)
+        open_tile(2, 6, 7)
         routed_both(2, 0)
         routed_both(2, 1)
         widen_on_scalar(1, 0, 0)
@@ -570,10 +598,10 @@ def tile_expert_pair_project_s3_kernel(
         quantize(("act", 1, 2))
         turn(("act", 2, 2), 0)
         turn(("act", 3, 0), 1)
-        interleave(1, 1, on_vector, slice(0, BANK // 2))
+        interleave(1, 1, on_vector, slice(0, 256))
         collect(("act", 2, 2), on_scalar)
-        interleave(1, 1, on_scalar, slice(BANK // 2, BANK))
         collect(("act", 3, 0), on_scalar)
+        interleave(1, 1, on_scalar, slice(256, 512))
         apply_gate(3, (1,))
         shared_pass(0, 0, 0)
         shared_pass(0, 1, 0)
@@ -582,6 +610,7 @@ def tile_expert_pair_project_s3_kernel(
         shared_pass(1, 1, 0)
         shared_pass(1, 0, 1)
         quantize(("act", 2, 2))
+        quantize(("act", 3, 0))
         scale_pair(0, 0)
         quantize_ws(1, 1)
         scale_pair(1, 0)
@@ -597,7 +626,7 @@ def tile_expert_pair_project_s3_kernel(
         shared_pass(2, 1, 1)
         gate_on_scalar(4, 1)
         order_hs(4, on_scalar)
-        quantize_routed(3)
+        quantize(("act", 3, 1))
         quantize(("act", 3, 2))
         scale_pair(0, 1)
         apply_gate(4, (0,))

from contextlib import ExitStack

import concourse.mybir as mybir
from concourse.masks import make_identity

TOKENS, SHARED, ROUTED, CHANNELS, FEATURES = 1024, 1024, 2048, 1024, 1536

FLOPS = 2 * TOKENS * CHANNELS * (SHARED + ROUTED) + 2 * TOKENS * CHANNELS * FEATURES

F32 = mybir.dt.float32
BF16 = mybir.dt.bfloat16
I32 = mybir.dt.int32
U32 = mybir.dt.uint32
U8 = mybir.dt.uint8
FP8 = mybir.dt.float8_e4m3fn
FP8X4 = mybir.dt.float8_e4m3fn_x4
FP4X4 = mybir.dt.float4_e2m1fn_x4
MULT = mybir.AluOpType.mult
ADD = mybir.AluOpType.add
COPY = mybir.ActivationFunctionType.Copy

P = 128
PACK = 4
K_PASS = P * PACK
UNIT = 2 * K_PASS
BANK = 512
BANKS = 8
TILES = TOKENS // P
R_PASSES = ROUTED // K_PASS
S_PASSES = SHARED // K_PASS
R_UNITS = ROUTED // UNIT
HALVES = CHANNELS // BANK
OUT_BANKS = FEATURES // BANK

OPENING = 3
QUAD = 32
QUADS = P // QUAD
ON_VECTOR = 6
GATED_ON_SCALAR = 2
LAG = 3


def tile_expert_pair_project_s3_kernel(
    tc, hs, hr, gate, ws_bytes, ws_scale, wr_words, wr_scales, gain, resid, wo_words, wo_scales, out
):
    nc = tc.nc
    with ExitStack() as ctx:
        keep = ctx.enter_context(tc.tile_pool(name="keep", bufs=1))
        work = ctx.enter_context(tc.tile_pool(name="work", bufs=3))
        psum = ctx.enter_context(tc.psum_pool(name="psum", bufs=1))
        ctx.enter_context(tc.manual_schedule())

        hs_rows = hs.rearrange("(p i) k -> p i k", i=TILES)
        hr_rows = hr.rearrange("(p i) k -> p i k", i=TILES)
        resid_rows = resid.rearrange("(p i) d -> p i d", i=TILES)
        out_rows = out.rearrange("(p i) n -> p i n", i=TILES)

        gate_sb = keep.tile([P, TILES], BF16, name="gate_sb")
        gate_f32 = keep.tile([P, TILES], F32, name="gate_f32")
        gain_sb = keep.tile([P, CHANNELS], BF16, name="gain_sb", align_bytes=256)
        hs_pairs = [keep.tile([P, 2, SHARED], BF16, name="hs%d" % j, align_bytes=256) for j in range(TILES // 2)]
        hs_sb = [hs_pairs[i // 2][:, i % 2, :] for i in range(TILES)]
        hr_sb = [keep.tile([P, ROUTED], BF16, name="hr%d" % i, align_bytes=256) for i in range(ON_VECTOR)]
        late = TILES - ON_VECTOR
        hr_quads = [keep.tile([P, late * R_PASSES, P], BF16, name="hr_quad%d" % b, align_bytes=256) for b in range(QUADS)]
        gate_quads = keep.tile([P, QUADS, TILES], BF16, name="gate_quads")
        gate_wide = keep.tile([P, QUADS, TILES], F32, name="gate_wide")
        staged = {}
        flipped = {}
        resid_sb = [keep.tile([P, CHANNELS], BF16, name="resid%d" % i, align_bytes=256) for i in range(TILES)]
        wr_sb = [keep.tile([P, 2 * CHANNELS], U8, name="wr%d" % g, align_bytes=256) for g in range(R_PASSES)]
        wo_sb = keep.tile([P, HALVES, 2 * FEATURES], U8, name="wo_sb", align_bytes=256)
        def shifted(name, rows, width):
            whole = keep.tile([P, rows * width // 4], I32, name=name, align_bytes=256)
            return whole[:].rearrange("p (g n) -> p g n", g=rows)

        wr_planes = [shifted("wr_planes%d" % b, 2, CHANNELS) for b in range(R_UNITS)]
        wo_planes = shifted("wo_planes", HALVES, FEATURES)
        ws_scale_sb = keep.tile([P, S_PASSES, PACK], F32, name="ws_scale_sb")
        ws_raw = [
            [keep.tile([P, 2, CHANNELS], U8, name="ws_raw%d%d" % (g, j), align_bytes=256) for j in range(2)] for g in range(S_PASSES)
        ]

        ws_parts = [(g, h) for g in range(S_PASSES) for h in range(HALVES)]
        ws_wide = {gh: keep.tile([P, PACK, BANK], BF16, name="ws_wide%d%d" % gh) for gh in ws_parts}
        ws_codes = {gh: keep.tile([P, BANK], U32, name="ws_codes%d%d" % gh, align_bytes=256) for gh in ws_parts}
        ws_planes = {
            gh: keep.tile([P, BANK], U8, name="ws_planes%d%d" % gh, align_bytes=256)[:] for gh in ws_parts
        }
        ws_packed = {}

        ident = keep.tile([P, P], F32, name="ident")

        units = {}
        z_rows = {}
        turned = {}
        grouped = {}
        operands = {}
        pair_banks = {}
        passes_done = {}
        scaled_pairs = {}
        out_banks = {}
        results = {}

        def load_hr(i, cols=slice(0, ROUTED)):
            nc.sync.dma_start(out=hr_sb[i][:, cols], in_=hr_rows[:, i, cols])

        def load_quads(b):
            pieces = hr.rearrange("(b r i) (g q c) -> q b r (i g) c", b=QUADS, r=QUAD, g=R_PASSES, q=QUADS)
            for q in (0, 2, 1, 3):
                nc.sync.dma_start(
                    out=hr_quads[b][q * QUAD : (q + 1) * QUAD, :, :], in_=pieces[q, b][:, ON_VECTOR * R_PASSES :, :]
                )

        def load_gate_quads():
            for q in range(QUADS):
                nc.sync.dma_start(
                    out=gate_quads[q * QUAD : (q + 1) * QUAD, :, :], in_=gate.rearrange("(b r i) -> r b i", b=QUADS, r=QUAD)
                )

        def load_hs(j):
            nc.sync.dma_start(out=hs_pairs[j][:], in_=hs_rows[:, 2 * j : 2 * j + 2, :])

        def load_resid(i):
            nc.sync.dma_start(out=resid_sb[i][:], in_=resid_rows[:, i, :])

        def load_ws(g, j):
            by_pass = ws_bytes.rearrange("(g p t) n -> g p t n", p=P, t=PACK)
            nc.sync.dma_start(out=ws_raw[g][j][:], in_=by_pass[g][:, 2 * j : 2 * j + 2, :])

        def load_wr(g):
            nc.sync.dma_start(out=wr_sb[g][:], in_=wr_words[g])

        def load_planes(planes, scales):
            as_int = scales.bitcast(I32)
            for r in range(4):
                nc.sync.dma_start(out=planes[r:P:32, :, :], in_=as_int[:, r:16:4, :].rearrange("g q n -> q g n"))

        def split(ap):
            return ap.rearrange("p (w u e) -> p u w e", u=2, e=2)

        def apply_gate(i, parts=(0, 1)):
            width = len(parts) * UNIT
            routed = work.tile([P, width], BF16, name="routed%d" % len(parts), bufs=2 if len(parts) == 1 else 1)
            source = hr_sb[i][:, parts[0] * UNIT : parts[0] * UNIT + width]
            nc.vector.tensor_scalar(
                out=routed[:, 0:width].rearrange("p (u w e) -> p w u e", u=2, e=2),
                in0=source.rearrange("p (w u e) -> p w u e", u=2, e=2),
                scalar1=gate_sb[:, i : i + 1],
                scalar2=None,
                op0=MULT,
            )
            words = routed[:, 0:width].bitcast(F32).rearrange("p (u w) -> p u w", u=2)
            for n, b in enumerate(parts):
                units["act", i, b] = words[:, :, 2 * P * n : 2 * P * (n + 1)]

        def gate_quad(i, groups):
            if i not in staged:
                staged[i] = work.tile([P, QUADS, K_PASS], BF16, name="staged", bufs=1, align_bytes=64)
            first = (i - ON_VECTOR) * R_PASSES
            for b in groups:
                source = hr_quads[b][:, first : first + R_PASSES, :].rearrange("p g (w u e) -> p (g w) u e", u=2, e=2)
                target = staged[i][:, b, :].rearrange("p (u w e) -> p w u e", u=2, e=2)
                factor = gate_wide[:, b, i : i + 1]
                if b < GATED_ON_SCALAR:
                    nc.scalar.activation(out=target, in_=source, func=COPY, scale=factor)
                else:
                    nc.vector.tensor_scalar(out=target, in0=source, scalar1=factor, scalar2=None, op0=MULT)

        def flip(i):
            flipped[i] = work.tile([P, UNIT], F32, name="flipped", bufs=1, align_bytes=64)
            words = staged[i][:].rearrange("p b k -> p (b k)").bitcast(F32)
            nc.vector.transpose(out=flipped[i][:], in_=words)

        def collect_flipped(i):
            grouped["routed", i] = work.tile([P, ROUTED], BF16, name="grouped_r", bufs=2, align_bytes=256)
            nc.scalar.copy(
                out=grouped["routed", i][:].bitcast(F32).rearrange("p (g b r u) -> p g b r u", g=R_PASSES, b=QUADS, u=2),
                in_=flipped[i][:].rearrange("p (b u g r) -> p g b r u", b=QUADS, u=2, g=R_PASSES),
            )

        def gate_on_scalar(i, b):
            routed = work.tile([P, UNIT], BF16, name="routed1", bufs=2)
            nc.scalar.activation(
                out=routed[:, 0:UNIT].rearrange("p (u w e) -> p w u e", u=2, e=2),
                in_=hr_sb[i][:, b * UNIT : (b + 1) * UNIT].rearrange("p (w u e) -> p w u e", u=2, e=2),
                func=COPY,
                scale=gate_f32[:, i : i + 1],
            )
            units["act", i, b] = routed[:, 0:UNIT].bitcast(F32).rearrange("p (u w) -> p u w", u=2)

        def order_hs(i, copy):
            ordered = work.tile([P, 2, 2 * P], F32, name="ordered", bufs=3)
            copy(out=ordered[:].rearrange("p u w -> p w u"), in_=hs_sb[i].bitcast(F32).rearrange("p (w u) -> p w u", u=2))
            units["act", i, R_UNITS] = ordered[:]

        def bank_tile(k, shape, dtype=F32):
            return psum.tile(shape, dtype, name="bank%d" % k)

        def turn(key, k):
            bank = bank_tile(k, [P, 2, 2, P])
            for g in range(2):
                for u in range(2):
                    nc.tensor.transpose(bank[:, g, u, :], units[key][:, u, g * P : (g + 1) * P], ident[:])
            turned[key] = bank

        def collect(key, copy):
            if key[0] == "act" and key[2] < R_UNITS and key[1] > OPENING:
                if key[2] == 0:
                    grouped["routed", key[1]] = work.tile([P, ROUTED], BF16, name="grouped_r", bufs=2, align_bytes=256)
                rows = grouped["routed", key[1]][:, key[2] * UNIT : (key[2] + 1) * UNIT]
            else:
                single = work.tile([P, UNIT], BF16, name="grouped", bufs=4, align_bytes=256)
                rows = single[:]
            copy(
                out=rows.bitcast(F32).rearrange("p (g r u) -> p g r u", g=2, u=2),
                in_=turned[key][:].rearrange("p g u r -> p g r u"),
            )
            grouped[key] = rows

        def quantize(key):
            codes = work.tile([P, 2 * P], U32, name="codes", bufs=8, align_bytes=256)
            planes = work.tile([P, 2 * P], U8, name="planes", bufs=8, align_bytes=256)
            nc.vector.quantize_mx(out=codes[:].bitcast(FP8X4), scales=planes[:], in_=grouped[key])
            operands[key] = (codes[:], planes[:])

        def turn_pass(key, g, k):
            bank = bank_tile(k, [P, 2, P])
            for u in range(2):
                nc.tensor.transpose(bank[:, u, :], units[key][:, u, g * P : (g + 1) * P], ident[:])
            turned[key, g] = bank

        def collect_pass(key, g, copy):
            rows = work.tile([P, K_PASS], BF16, name="grouped_pass", bufs=2, align_bytes=256)
            copy(out=rows[:].bitcast(F32).rearrange("p (r u) -> p r u", u=2), in_=turned[key, g][:].rearrange("p u r -> p r u"))
            grouped[key, g] = rows

        def quantize_pass(key, g):
            if g == 0:
                codes = work.tile([P, 2 * P], U32, name="codes", bufs=8, align_bytes=256)
                planes = work.tile([P, 2 * P], U8, name="planes", bufs=8, align_bytes=256)
                operands[key] = (codes[:], planes[:])
            codes, planes = stationary(key, g)
            nc.vector.quantize_mx(out=codes, scales=planes, in_=grouped[key, g][:])

        def quantize_routed(i):
            codes = work.tile([P, 4 * P], U32, name="codes_r", bufs=4, align_bytes=256)
            planes = work.tile([P, 4 * P], U8, name="planes_r", bufs=4, align_bytes=256)
            nc.vector.quantize_mx(out=codes[:].bitcast(FP8X4), scales=planes[:], in_=grouped["routed", i][:])
            for b in range(R_UNITS):
                cols = slice(2 * P * b, 2 * P * (b + 1))
                operands["act", i, b] = (codes[:, cols], planes[:, cols])

        def stationary(key, g):
            codes, planes = operands[key]
            cols = slice(g * P, (g + 1) * P)
            return codes[:, cols].bitcast(FP8X4), planes[:, cols]

        def widen_on_vector(g, h, t):
            cols = slice(h * BANK, (h + 1) * BANK)
            nc.vector.tensor_scalar(
                out=ws_wide[g, h][:, t, :],
                in0=ws_raw[g][t // 2][:, t % 2, cols].bitcast(FP8),
                scalar1=ws_scale_sb[:, g, t : t + 1],
                scalar2=None,
                op0=MULT,
            )

        def widen_on_scalar(g, h, t):
            cols = slice(h * BANK, (h + 1) * BANK)
            nc.scalar.activation(
                out=ws_wide[g, h][:, t, :],
                in_=ws_raw[g][t // 2][:, t % 2, cols].bitcast(FP8),
                func=COPY,
                scale=ws_scale_sb[:, g, t : t + 1],
            )

        def interleave(g, h, copy, cols=slice(0, BANK)):
            if (g, h) not in ws_packed:
                ws_packed[g, h] = work.tile([P, BANK, PACK], BF16, name="packed", bufs=2, align_bytes=256)
            copy(
                out=ws_packed[g, h][:, cols, :].rearrange("p (c i) t -> p c t i", i=4),
                in_=ws_wide[g, h][:, :, cols].rearrange("p t (c i) -> p c t i", i=4),
            )

        def quantize_ws(g, h):
            nc.vector.quantize_mx(
                out=ws_codes[g, h][:].bitcast(FP8X4),
                scales=ws_planes[g, h][:],
                in_=ws_packed[g, h][:].rearrange("p n t -> p (n t)"),
            )

        def open_pair(i, h, k):
            pair_banks[i, h] = bank_tile(k, [P, BANK])

        def flags(i, h):
            passes_done[i, h] = passes_done.get((i, h), 0) + 1
            return passes_done[i, h] == 1, passes_done[i, h] == R_PASSES + S_PASSES

        def routed_pass(i, h, g):
            start, stop = flags(i, h)
            codes, planes = stationary(("act", i, g // 2), g % 2)
            nc.tensor.matmul_mx(
                out=pair_banks[i, h][:],
                lhsT=codes,
                lhsT_scale=planes,
                rhs=wr_sb[g][:, 2 * h * BANK : 2 * (h + 1) * BANK].bitcast(FP4X4),
                rhs_scale=wr_planes[g // 2][:, g % 2, h * BANK // 4 : (h + 1) * BANK // 4].bitcast(U8),
                start=start,
                stop=stop,
            )

        def shared_pass(i, h, g):
            start, stop = flags(i, h)
            codes, planes = stationary(("act", i, R_UNITS), g)
            nc.tensor.matmul_mx(
                out=pair_banks[i, h][:],
                lhsT=codes,
                lhsT_scale=planes,
                rhs=ws_codes[g, h][:].bitcast(FP8X4),
                rhs_scale=ws_planes[g, h][:],
                start=start,
                stop=stop,
            )

        def routed_unit(i, b):
            for g in (2 * b, 2 * b + 1):
                for h in range(HALVES):
                    routed_pass(i, h, g)

        def shared_unit(i):
            for g in range(S_PASSES):
                for h in range(HALVES):
                    shared_pass(i, h, g)

        def half_pair(i, h, k):
            open_pair(i, h, k)
            for g in range(R_PASSES):
                routed_pass(i, h, g)
            for g in range(S_PASSES):
                shared_pass(i, h, g)

        def quarter_pair(i, cols, k):
            bank = bank_tile(k, [P, cols.stop - cols.start])
            h, inside = cols.start // BANK, slice(cols.start % BANK, (cols.stop - 1) % BANK + 1)
            for g in range(R_PASSES + S_PASSES):
                codes, planes = stationary(("act", i, g // 2), g % 2)
                if g < R_PASSES:
                    rhs = wr_sb[g][:, 2 * cols.start : 2 * cols.stop].bitcast(FP4X4)
                    rhs_scale = wr_planes[g // 2][:, g % 2, cols.start // 4 : cols.stop // 4].bitcast(U8)
                else:
                    rhs = ws_codes[g - R_PASSES, h][:, inside].bitcast(FP8X4)
                    rhs_scale = ws_planes[g - R_PASSES, h][:, inside]
                nc.tensor.matmul_mx(
                    out=bank[:],
                    lhsT=codes,
                    lhsT_scale=planes,
                    rhs=rhs,
                    rhs_scale=rhs_scale,
                    start=(g == 0),
                    stop=(g == R_PASSES + S_PASSES - 1),
                )
            pair_banks[i, cols.start] = bank

        def scale_quarter(i, cols):
            nc.vector.tensor_tensor(
                out=scaled_pairs[i][:, cols], in0=pair_banks[i, cols.start][:], in1=gain_sb[:, cols], op=MULT
            )

        def add_quarter(i, cols):
            words = slice(cols.start // PACK, cols.stop // PACK)
            nc.vector.tensor_tensor(
                out=z_rows[i][:].rearrange("p (u w e) -> p u w e", u=2, e=2)[:, :, words, :],
                in0=split(scaled_pairs[i][:, cols]),
                in1=split(resid_sb[i][:, cols]),
                op=ADD,
            )

        def scale_pair(i, h):
            if (i, 1 - h) not in scaled_pairs:
                scaled_pairs[i] = work.tile([P, CHANNELS], F32, name="scaled", bufs=3)
            scaled_pairs[i, h] = True
            channels = slice(h * BANK, (h + 1) * BANK)
            nc.vector.tensor_tensor(
                out=scaled_pairs[i][:, channels], in0=pair_banks[i, h][:], in1=gain_sb[:, channels], op=MULT
            )

        def add_resid(i, halves=(0, 1)):
            if halves[0] == 0:
                z_rows[i] = work.tile([P, UNIT], BF16, name="z", bufs=4)
                units["z", i] = z_rows[i][:].bitcast(F32).rearrange("p (u w) -> p u w", u=2)
            channels = slice(halves[0] * BANK, (halves[-1] + 1) * BANK)
            words = slice(halves[0] * P, (halves[-1] + 1) * P)
            nc.vector.tensor_tensor(
                out=z_rows[i][:].rearrange("p (u w e) -> p u w e", u=2, e=2)[:, :, words, :],
                in0=split(scaled_pairs[i][:, channels]),
                in1=split(resid_sb[i][:, channels]),
                op=ADD,
            )

        def project_pass(i, cols, g, k=None):
            if g == 0:
                out_banks[i, cols.start] = bank_tile(k, [P, cols.stop - cols.start])
            codes, planes = stationary(("z", i), g)
            nc.tensor.matmul_mx(
                out=out_banks[i, cols.start][:],
                lhsT=codes,
                lhsT_scale=planes,
                rhs=wo_sb[:, g, 2 * cols.start : 2 * cols.stop].bitcast(FP4X4),
                rhs_scale=wo_planes[:, g, cols.start // 4 : cols.stop // 4].bitcast(U8),
                start=(g == 0),
                stop=(g == HALVES - 1),
            )

        def empty(i, cols, copy):
            if cols.start == 0:
                results[i] = work.tile([P, FEATURES], F32, name="result", bufs=3, align_bytes=256)
            copy(out=results[i][:, cols], in_=out_banks[i, cols.start][:])

        def project(i, n, k, copy=nc.scalar.copy):
            cols = slice(n * BANK, (n + 1) * BANK)
            for g in range(HALVES):
                project_pass(i, cols, g, k)
            empty(i, cols, copy)

        def store(i, cols=slice(0, FEATURES)):
            nc.sync.dma_start(out=out_rows[:, i, cols], in_=results[i][:, cols])

        primer = keep.tile([P, 2], F32, name="primer")
        nc.vector.memset(primer[:], 0.0)
        for b in range(R_UNITS):
            nc.vector.memset(wr_planes[b][:], 0)
        nc.vector.memset(wo_planes[:], 0)
        make_identity(nc, ident[:])
        nc.scalar.activation(out=primer[:, 1:2], in_=primer[:, 0:1], func=COPY)
        first, second = slice(0, UNIT), slice(UNIT, ROUTED)
        on_vector, on_scalar = nc.vector.tensor_copy, nc.scalar.copy

        def load_small():
            nc.sync.dma_start(out=gate_sb[:], in_=gate.rearrange("(p i) -> p i", i=TILES))

        def load_scale():
            nc.sync.dma_start(out=ws_scale_sb[:], in_=ws_scale.rearrange("(g p t) o -> p g (t o)", p=P, t=PACK))

        def load_gain():
            nc.sync.dma_start(out=gain_sb[:], in_=gain.partition_broadcast(P))

        def load_wo():
            load_planes(wo_planes, wo_scales)
            nc.sync.dma_start(out=wo_sb[:], in_=wo_words.rearrange("g p n -> p g n"))

        def routed_both(i, g):
            for h in range(HALVES):
                routed_pass(i, h, g)

        def routed_half(i, h):
            for g in range(R_PASSES):
                routed_pass(i, h, g)

        def shared_half(i, h):
            for g in range(S_PASSES):
                shared_pass(i, h, g)

        def open_tile(i, k0, k1):
            open_pair(i, 0, k0)
            open_pair(i, 1, k1)

        def warm(copies, k):
            bank = bank_tile(k, [P, copies, P])
            moving = ident[:].unsqueeze(1).to_broadcast([P, copies, P])
            nc.tensor.matmul(bank[:], lhsT=ident[:], rhs=moving, start=True, stop=True)

        def banks_of(i):
            return [slice(n * BANK, (n + 1) * BANK) for n in range(OUT_BANKS)]

        def project_and_store(i, cols, copy, k):
            project_pass(i, cols, 0, k)
            project_pass(i, cols, 1)
            empty(i, cols, copy)
            store(i, cols)

        load_scale()
        load_ws(0, 0)
        load_small()
        load_hr(0, first)
        load_ws(0, 1)
        load_hr(0, second)
        load_hr(1)
        load_hr(2)
        load_planes(wr_planes[0], wr_scales[0 : 2])
        load_wr(0)
        load_wr(1)
        load_ws(1, 0)
        load_ws(1, 1)
        load_planes(wr_planes[1], wr_scales[2 : 4])
        load_wr(2)
        load_hs(0)
        load_wr(3)
        load_hs(1)
        load_hr(3, first)
        load_hr(3, second)
        load_gain()
        load_resid(0)
        load_hr(4)
        load_hs(2)
        load_resid(1)
        load_wo()
        load_hr(5)
        load_resid(2)
        load_hs(3)
        load_resid(3)
        load_gate_quads()
        load_quads(0)
        load_quads(1)
        load_quads(2)
        load_quads(3)
        load_resid(4)
        load_resid(5)
        load_resid(6)
        load_resid(7)
        warm(4, 7)
        widen_on_vector(0, 0, 0)
        widen_on_scalar(0, 1, 0)
        widen_on_vector(0, 0, 1)
        apply_gate(0, (0,))
        turn(("act", 0, 0), 0)
        warm(2, 7)
        widen_on_scalar(0, 1, 1)
        nc.scalar.copy(out=gate_f32[:], in_=gate_sb[:])
        widen_on_vector(0, 0, 2)
        collect(("act", 0, 0), on_scalar)
        widen_on_vector(0, 0, 3)
        apply_gate(0, (1,))
        turn(("act", 0, 1), 1)
        warm(2, 7)
        widen_on_scalar(0, 1, 2)
        interleave(0, 0, on_vector, slice(0, 256))
        apply_gate(1, (0,))
        apply_gate(1, (1,))
        collect(("act", 0, 1), on_scalar)
        turn(("act", 1, 0), 4)
        turn(("act", 1, 1), 5)
        warm(2, 3)
        widen_on_scalar(0, 1, 3)
        quantize(("act", 0, 0))
        apply_gate(2, (0,))
        apply_gate(2, (1,))
        collect(("act", 1, 0), on_scalar)
        collect(("act", 1, 1), on_scalar)
        turn(("act", 2, 0), 6)
        turn(("act", 2, 1), 7)
        quantize(("act", 0, 1))
        quantize(("act", 1, 0))
        collect(("act", 2, 0), on_scalar)
        collect(("act", 2, 1), on_scalar)
        interleave(0, 0, on_vector, slice(256, 512))
        open_tile(0, 2, 3)
        routed_both(0, 0)
        routed_both(0, 1)
        open_tile(1, 4, 5)
        routed_both(1, 0)
        routed_both(1, 1)
        quantize(("act", 2, 0))
        open_tile(2, 6, 7)
        routed_both(2, 0)
        routed_both(2, 1)
        widen_on_scalar(1, 0, 0)
        widen_on_scalar(1, 0, 1)
        widen_on_scalar(1, 0, 2)
        widen_on_scalar(1, 0, 3)
        interleave(0, 1, on_vector)
        quantize(("act", 1, 1))
        quantize(("act", 2, 1))
        quantize_ws(0, 0)
        order_hs(0, on_vector)
        order_hs(1, on_vector)
        routed_both(0, 2)
        routed_both(1, 2)
        routed_both(2, 2)
        widen_on_scalar(1, 1, 0)
        widen_on_scalar(1, 1, 1)
        interleave(1, 0, on_vector)
        turn(("act", 0, 2), 0)
        turn(("act", 1, 2), 1)
        widen_on_scalar(1, 1, 2)
        collect(("act", 0, 2), on_scalar)
        collect(("act", 1, 2), on_scalar)
        widen_on_scalar(1, 1, 3)
        order_hs(3, on_scalar)
        routed_both(0, 3)
        routed_both(1, 3)
        routed_both(2, 3)
        quantize_ws(0, 1)
        order_hs(2, on_vector)
        apply_gate(3, (0,))
        quantize(("act", 0, 2))
        quantize_ws(1, 0)
        quantize(("act", 1, 2))
        turn(("act", 2, 2), 0)
        turn(("act", 3, 0), 1)
        interleave(1, 1, on_vector, slice(0, 256))
        collect(("act", 2, 2), on_scalar)
        collect(("act", 3, 0), on_scalar)
        interleave(1, 1, on_scalar, slice(256, 512))
        apply_gate(3, (1,))
        shared_pass(0, 0, 0)
        shared_pass(0, 1, 0)
        shared_pass(0, 0, 1)
        shared_pass(1, 0, 0)
        shared_pass(1, 1, 0)
        shared_pass(1, 0, 1)
        quantize(("act", 2, 2))
        quantize(("act", 3, 0))
        scale_pair(0, 0)
        quantize_ws(1, 1)
        scale_pair(1, 0)
        turn(("act", 3, 1), 0)
        turn(("act", 3, 2), 1)
        collect(("act", 3, 1), on_scalar)
        collect(("act", 3, 2), on_scalar)
        shared_pass(2, 0, 0)
        shared_pass(2, 1, 0)
        shared_pass(2, 0, 1)
        shared_pass(0, 1, 1)
        shared_pass(1, 1, 1)
        shared_pass(2, 1, 1)
        gate_on_scalar(4, 1)
        order_hs(4, on_scalar)
        quantize(("act", 3, 1))
        quantize(("act", 3, 2))
        scale_pair(0, 1)
        apply_gate(4, (0,))
        add_resid(0)
        scale_pair(2, 0)
        half_pair(3, 0, 2)
        turn(("act", 4, 0), 1)
        turn(("act", 4, 1), 0)
        turn(("act", 4, 2), 4)
        turn(("z", 0), 3)
        collect(("act", 4, 0), on_scalar)
        collect(("z", 0), on_scalar)
        collect(("act", 4, 1), on_scalar)
        collect(("act", 4, 2), on_scalar)
        scale_pair(1, 1)
        scale_pair(2, 1)
        quantize(("z", 0))
        half_pair(3, 1, 6)
        scale_pair(3, 0)
        quantize_routed(4)
        order_hs(5, on_scalar)
        project(0, 0, 5)
        project(0, 1, 7)
        project(0, 2, 3)
        store(0)
        quantize(("act", 4, 2))
        add_resid(1)
        apply_gate(5)

        taken = []
        ring = (1, 0, 4, 2, 5, 7, 3, 6)

        def next_bank():
            taken.append(ring[len(taken) % BANKS])
            return taken[-1]

        def turn_next(key):
            turn(key, next_bank())
            collect(key, on_scalar)

        last = TILES - 1
        half_pair(4, 0, next_bank())
        scale_pair(3, 1)
        add_resid(2)
        nc.scalar.copy(out=gate_wide[:], in_=gate_quads[:])
        turn(("z", 1), next_bank())
        turn(("act", 5, 0), next_bank())
        turn(("act", 5, 1), next_bank())
        turn(("act", 5, 2), next_bank())
        collect(("z", 1), on_scalar)
        collect(("act", 5, 0), on_scalar)
        collect(("act", 5, 1), on_scalar)
        collect(("act", 5, 2), on_scalar)
        scale_pair(4, 0)
        quantize(("z", 1))
        half_pair(4, 1, next_bank())
        quantize_routed(5)
        quantize(("act", 5, 2))
        order_hs(6, on_scalar)
        order_hs(7, on_scalar)
        scale_pair(4, 1)
        add_resid(3)
        project(1, 0, next_bank())
        gate_quad(6, range(GATED_ON_SCALAR))
        gate_quad(6, range(GATED_ON_SCALAR, QUADS))
        project(1, 1, next_bank())
        project(1, 2, next_bank())
        store(1)
        flip(6)
        half_pair(5, 0, next_bank())
        turn(("z", 2), next_bank())
        turn(("act", 6, 2), next_bank())
        turn(("act", 7, 2), next_bank())
        turn(("z", 3), next_bank())
        collect(("z", 2), on_scalar)
        collect_flipped(6)
        collect(("act", 6, 2), on_scalar)
        scale_pair(5, 0)
        quantize(("z", 2))
        add_resid(4)
        half_pair(5, 1, next_bank())
        gate_quad(7, range(GATED_ON_SCALAR))
        quantize_routed(6)
        quantize(("act", 6, 2))
        collect(("act", 7, 2), on_scalar)
        collect(("z", 3), on_scalar)
        project(2, 0, next_bank())
        project(2, 1, next_bank())
        project(2, 2, next_bank())
        store(2)
        gate_quad(7, range(GATED_ON_SCALAR, QUADS))
        scale_pair(5, 1)
        flip(7)
        half_pair(6, 0, next_bank())
        collect_flipped(7)
        quantize(("z", 3))
        add_resid(5)
        scale_pair(6, 0)
        half_pair(6, 1, next_bank())
        quantize_routed(7)
        quantize(("act", 7, 2))
        scale_pair(6, 1)
        project(3, 0, next_bank())
        project(3, 1, next_bank())
        project(3, 2, next_bank())
        store(3)

        def banks_of(i):
            return [slice(n * BANK, (n + 1) * BANK) for n in range(OUT_BANKS)]

        def project_and_store(i, cols, copy):
            project_pass(i, cols, 0, next_bank())
            project_pass(i, cols, 1)
            empty(i, cols, copy)
            store(i, cols)

        head, middle, end = banks_of(last)
        for j in (last - 3, last - 2):
            turn_next(("z", j))
        half_pair(last, 0, next_bank())
        add_resid(last - 1)
        quantize(("z", last - 3))
        quantize(("z", last - 2))
        scale_pair(last, 0)
        for cols in (head, middle, end):
            project_and_store(last - 3, cols, on_scalar)
        add_resid(last, (0,))
        turn(("z", last - 1), next_bank())
        collect(("z", last - 1), on_vector)
        project_and_store(last - 2, head, on_scalar)
        quantize(("z", last - 1))
        quarters = (slice(BANK, BANK + BANK // 2), slice(BANK + BANK // 2, CHANNELS))
        for cols in quarters:
            quarter_pair(last, cols, next_bank())
            scale_quarter(last, cols)
            add_quarter(last, cols)
        project_and_store(last - 2, middle, on_scalar)
        project_and_store(last - 2, end, on_vector)
        project_and_store(last - 1, head, on_scalar)
        for g in range(HALVES):
            turn_pass(("z", last), g, next_bank())
        collect_pass(("z", last), 0, on_vector)
        collect_pass(("z", last), 1, on_scalar)
        for g in range(HALVES):
            quantize_pass(("z", last), g)
        project_and_store(last - 1, middle, on_scalar)
        project_and_store(last - 1, end, on_vector)
        project_and_store(last, head, on_scalar)
        project_and_store(last, middle, on_vector)
        project_and_store(last, end, on_scalar)
